import numpy as np, ml_dtypes
CORES = [23,119,17,113]
N = 4
BF = ml_dtypes.bfloat16
def gentries(a):
    return np.ascontiguousarray(a.reshape(8, 16, -1).transpose(0, 2, 1)).reshape(8, -1)
def gtable(e):
    e = np.asarray(e); return np.ascontiguousarray(e.reshape(8, -1, 16).transpose(0, 2, 1)).reshape(128, -1).astype(np.int32)
W, MA, J, P, T = 3072, 256, 768, 4, 3
def lanes(rng, big=False):
    jm = np.zeros((N, 8, MA), np.int64); lab = np.zeros((N, 8, J), np.int64); nx = np.zeros((N, 8, 16, J), np.int64)
    for q in range(N):
        for g in range(8):
            o = rng.permutation(J); p = rng.permutation(MA)
            tail = p[(MA * rng.random(J - MA) ** 2).astype(np.int64)]
            if big: tail[:] = p[0]
            lb = np.concatenate([np.arange(MA), tail]); s = np.argsort(lb, kind="stable"); cnt = np.bincount(lb, minlength=MA); st = np.add.accumulate(cnt) - cnt
            jm[q, g] = o[:MA]; lab[q, g, o] = lb
            nx[q, g][:, o] = o[s[st[lb] + (cnt[lb] * rng.random((16, J))).astype(np.int64)]]
            if big:
                pos = np.zeros(J, np.int64); pos[s] = np.arange(J) - st[lb[s]]
                nx[q, g][:8, o] = o[s[st[lb] + (pos + 1) % cnt[lb]]]
    return jm, lab, nx
def parts(rng, big=False):
    jm, lab, nx = lanes(rng, big); pal = rng.integers(0, W, (8, 16, MA, 6))
    ga = np.arange(8)[None, :, None, None]; ka = np.arange(16)[None, None, :, None]
    tool = np.where(rng.random((N, 8, 16, J)) < 0.75, pal[ga, ka, lab[:, :, None, :], rng.integers(0, 6, (N, 8, 16, J))], rng.integers(0, W, (N, 8, 16, J)))
    sh = (N, 8, 16, P, MA)
    name = np.where(rng.random(sh) < 0.8, pal[ga[..., None], ka[..., None], np.arange(MA), rng.integers(0, 6, sh)], rng.integers(0, W, sh))
    x = np.clip(rng.integers(0, 256, (N, 8, 1, W)) + rng.integers(-64, 65, (N, 8, 16, W)), 0, 255)
    lm = np.clip(rng.integers(64, 257, (N, 8, 1, J)) + rng.integers(-48, 49, (N, 8, 16, J)), 0, 255)
    return {"jm": jm, "nx": nx, "tool": tool, "name": name, "f": rng.integers(0, J, sh), "x": x, "lm": lm, "sd": rng.integers(0, 256, (N, 8, 16, W)), "rt": rng.integers(0, 65, (N, 8, 16, T))}
def full(a):
    return np.ascontiguousarray(a.reshape(N, 128, -1))
def pack(v):
    b = {k: full(v[k]).astype(np.float32).astype(BF) for k in ("x", "sd", "lm", "rt")}
    return {"xw": b["x"], "sd": b["sd"], "jt": full(4096 * v["nx"] + v["tool"]).astype(np.int32), "lm": b["lm"], "rt": b["rt"],
            "pk": full(4096 * v["f"] + v["name"]).astype(np.int32), "jm": np.stack([gtable(a) for a in v["jm"]])}
def setup_inputs(rng):
    return pack(parts(rng))
def setup_inputs_ties(rng):
    v = parts(rng)
    n = rng.choice(np.array([0, 7, 8, 9, 10, 16]), (N, 8, 1, W)); r = np.argsort(rng.random((N, 8, 16, W)), axis=2)
    v["x"] = 100 + (r < n).astype(np.int64); v["lm"] = np.full((N, 8, 16, J), 100); v["rt"] = rng.integers(0, 3, (N, 8, 16, T))
    v["f"] = rng.choice(np.array([0, J // 2, J - 1]), (N, 8, 16, P, MA))
    v["name"][:, :, :, 1] = np.where(rng.random((N, 8, 16, MA)) < 0.5, v["name"][:, :, :, 0], v["name"][:, :, :, 1])
    return pack(v)
def setup_inputs_crowd(rng):
    v = parts(rng); few = rng.integers(0, W, (8, 24)); ga = np.arange(8)[None, :, None, None]; m = np.arange(MA)
    v["tool"] = few[ga, rng.integers(0, 24, (N, 8, 16, J))]; v["name"] = few[ga[..., None], rng.integers(0, 24, (N, 8, 16, P, MA))]
    v["x"] = rng.choice(np.array([0, 3, 7, 8, 9, 128, 250, 254, 255]), (N, 8, 16, W)); v["rt"] = rng.choice(np.array([0, 1, 5, 64]), (N, 8, 16, T))
    other = np.setdiff1d(np.arange(W), few)
    for q in range(N):
        o = rng.permutation(8)
        g = o[0]; c, d = rng.permutation(other)[:2]
        v["lm"][q, g] = 255; v["tool"][q, g] = d; v["name"][q, g] = c; v["f"][q, g][:, 0] = J - 1; v["x"][q, g][:, c] = rng.integers(32, 256, 16)
        for g, w in ((o[1], 0), (o[2], 255)):
            c, d, e = rng.permutation(other)[:3]; m0 = int(rng.integers(1, 9))
            nm = np.where(m < m0, e, c); goes = (m == m0) == (w == 0)
            v["lm"][q, g] = 255; v["x"][q, g] = w; v["name"][q, g][0] = nm
            v["tool"][q, g][0, v["jm"][q, g]] = np.where(goes, nm, d)
            v["rt"][q, g] = rng.integers(17, 65, (16, T)) if w == 0 else rng.integers(0, 3, (16, T))
        g = o[3]; a = rng.permutation(W)[:17]; k0 = rng.integers(1, 8, MA)
        v["x"][q, g][:, a[0]] = rng.integers(0, 150, 16)
        v["x"][q, g][:, a[1:]] = rng.permuted(np.tile(rng.integers(150, 256, (16, 1)), (1, 16)), axis=0)
        v["tool"][q, g][:, v["jm"][q, g]] = np.where(np.arange(16)[:, None] < k0[None, :], a[0], a[1:][:, None])
    return pack(v)
def setup_inputs_ends(rng):
    v = parts(rng, True); e = np.array([0, 1, W - 2, W - 1])
    v["tool"] = np.where(rng.random((N, 8, 16, J)) < 0.5, rng.choice(e, (N, 8, 16, J)), v["tool"])
    v["name"] = np.where(rng.random((N, 8, 16, P, MA)) < 0.5, rng.choice(e, (N, 8, 16, P, MA)), v["name"])
    v["sd"] = np.where(rng.random((N, 8, 16, W)) < 0.5, rng.choice(np.array([0, 1, 255]), (N, 8, 16, W)), v["sd"])
    v["f"] = np.where(rng.random((N, 8, 16, P, MA)) < 0.5, rng.choice(np.array([0, J - 1]), (N, 8, 16, P, MA)), v["f"])
    return pack(v)
def setup_inputs_calm(rng):
    v = parts(rng); q = rng.permutation(N)
    v["lm"][q[0]] = 255; a = np.take_along_axis(v["tool"][q[0]], v["jm"][q[0]][:, None, :], 2)
    np.put_along_axis(v["name"][q[0]], rng.integers(0, P, (8, 16, 1, MA)), a[:, :, None, :], 2)
    v["lm"][q[1]] = 0; v["x"][q[1]] = np.maximum(v["x"][q[1]], 1)
    v["tool"][q[2]] = 2 * (v["tool"][q[2]] // 2); v["sd"][q[2]] = 2 * (v["sd"][q[2]] // 2); v["name"][q[2]] = 2 * (v["name"][q[2]] // 2) + 1
    return pack(v)
def setup_inputs_spread(rng):
    v = parts(rng)
    v["x"] = np.minimum((np.exp2(8 * rng.random((N, 8, 1, W))) * rng.random((N, 8, 16, W))).astype(np.int64), 255)
    v["lm"] = np.minimum((np.exp2(8 * rng.random((N, 8, 1, J))) * rng.random((N, 8, 16, J))).astype(np.int64), 255)
    v["rt"] = np.minimum(np.exp2(6 * rng.random((N, 8, 16, T))).astype(np.int64), 64)
    v["sd"] = np.minimum(np.exp2(8 * rng.random((N, 8, 16, W))).astype(np.int64), 255)
    v["tool"] = np.where(rng.random((N, 8, 16, J)) < 0.5, np.minimum((W * rng.random((N, 8, 16, J)) ** 3).astype(np.int64), W - 1), v["tool"])
    v["f"] = np.minimum((J * rng.random((N, 8, 16, P, MA)) ** 3).astype(np.int64), J - 1)
    return pack(v)
def check_inputs(d):
    bad = []
    for k, hi in (("xw", 255), ("sd", 255), ("lm", 255), ("rt", 64)):
        v = np.asarray(d[k]).astype(np.float64)
        if not np.all((v >= 0) & (v <= hi) & (v == np.floor(v))): bad.append("range of " + k)
    for k in ("jt", "pk"):
        v = np.asarray(d[k]).astype(np.int64)
        if np.min(v) < 0 or np.max(v) > 4096 * J - 1 or np.max(v & 4095) > W - 1: bad.append("range of " + k)
    if np.min(d["jm"]) < 0 or np.max(d["jm"]) > J - 1: bad.append("range of jm")
    if bad: return bad
    ok = True; nx = np.asarray(d["jt"]).astype(np.int64).reshape(N, 8, 16, J) >> 12
    for q in range(N):
        starts = gentries(np.asarray(d["jm"][q])).astype(np.int64)
        for g in range(8):
            fr = starts[g]; lab = np.full(J, -1)
            if len(np.unique(fr)) < MA: ok = False; continue
            lab[fr] = np.arange(MA)
            while len(fr):
                tg = nx[q, g][:, fr].reshape(-1); lb = np.tile(lab[fr], 16); new = lab[tg] < 0
                lab[tg[new]] = lb[new]
                if np.any(lab[tg] != lb): ok = False; break
                fr = np.unique(tg[new])
    if not ok: bad.append("lanes: a job can be reached from the starting jobs of two machines")
    return bad
def reference(xw, sd, jt, lm, rt, pk, jm):
    x = xw.astype(np.int64).reshape(N, 8, 16, W); s = sd.astype(np.int64).reshape(N, 8, 16, W); lim = lm.astype(np.int64).reshape(N, 8, 16, J); wr = rt.astype(np.int64).reshape(N, 8, 16, T)
    tab = jt.astype(np.int64).reshape(N, 8, 16, J); p = pk.astype(np.int64).reshape(N, 8, 16, P, MA)
    j = np.stack([gentries(a) for a in jm]).astype(np.int64)
    qa = np.arange(N)[:, None, None]; ga = np.arange(8)[None, :, None]
    for t in range(T):
        jj = np.ascontiguousarray(np.broadcast_to(j[:, :, None, :], (N, 8, 16, MA)))
        rec = np.take_along_axis(tab, jj, 3); a = rec & 4095; n = rec >> 12
        xa = np.take_along_axis(x, a.reshape(N, 8, 1, 16 * MA), 3).reshape(N, 8, 16, 16, MA)
        over = xa > np.take_along_axis(lim, jj, 3)[:, :, :, None, :]
        cond = np.add.reduce(over.astype(np.int64), axis=2) >= 9
        ks = np.argmax(np.add.reduce(xa, axis=2), axis=2)[:, :, None]
        b = a + np.take_along_axis(s, a, 3); b = np.where(b >= W, b - W, b)
        n2 = np.take_along_axis(tab, n, 3) >> 12
        a = np.where(cond, b, a); n = np.where(cond, n2, n)
        np.put_along_axis(tab, jj, 4096 * n + a, 3)
        eq = (p & 4095) == a[:, :, :, None]; hit = np.any(eq, axis=3)
        slot = np.where(hit, np.argmax(eq, axis=3), np.argmax(p >> 12, axis=3))[:, :, :, None]
        old = np.take_along_axis(p, slot, 3)[:, :, :, 0]
        send = np.where(hit, p[:, :, :, P - 1], old)
        np.put_along_axis(p, slot, (4096 * n + a)[:, :, :, None], 3)
        p[:, :, :, P - 1] = np.roll(send, 1, axis=0)
        v = np.take_along_axis(np.where(hit, a, old & 4095), ks, 2)[:, :, 0]; up = np.take_along_axis(hit, ks, 2)[:, :, 0]
        j = np.take_along_axis(n, ks, 2)[:, :, 0]
        low = np.full((N, 8, W), MA); np.minimum.at(low, (qa, ga, v), np.arange(MA)[None, None, :])
        wears = np.take_along_axis(up, np.minimum(low, MA - 1), 2)[:, :, None]
        x = np.where((low < MA)[:, :, None], np.where(wears, np.minimum(x + wr[:, :, :, t:t + 1], 255), np.maximum(x - 8, 0)), x)
    return {"yx": x.reshape(N, 128, W).astype(np.float32).astype(BF), "yp": p.reshape(N, 128, P * MA).astype(np.float32)}

@@ -1,0 +1,478 @@
+from concourse.mybir import AluOpType, ActivationFunctionType
+
+OP = AluOpType
+AF = ActivationFunctionType
+KD = (8, 9, 10, 11, 12, 13, 14, 15)
+KA = tuple(k for k in range(16) if k not in KD)
+XV = ((2, 3), (3,), (3,))
+BIG = 16777216.0
+
+
+def _s(shape, names, dtype, where="sbuf"):
+    return {n: (where, shape, dtype) for n in names.split()}
+
+
+SCRATCH = {}
+SCRATCH.update(_s([128, 3328], "X", "bfloat16"))
+SCRATCH.update(_s([128, 3072], "SD", "bfloat16"))
+SCRATCH.update(_s([128, 768], "JT TT NT", "int32"))
+SCRATCH.update(_s([128, 768], "LM GI SL", "bfloat16"))
+SCRATCH.update(_s([128, 768], "OUTP", "float32"))
+SCRATCH.update(_s([128, 4], "RT", "bfloat16"))
+SCRATCH.update(_s([128, 4], "RTF", "float32"))
+SCRATCH.update(_s([128, 8], "BB", "float32"))
+SCRATCH.update(_s([128, 8], "ROW8 IB", "bfloat16"))
+SCRATCH.update(_s([128, 1], "THR HB EB", "float32"))
+SCRATCH.update(_s([128, 16], "JM PI KI PG PQ", "int32"))
+SCRATCH.update(_s([128, 16], "J0 J1 VL OL", "uint16"))
+SCRATCH.update(_s([128, 16], "VLF PF CK KM LTM", "float32"))
+SCRATCH.update(_s([128, 1024], "PK Q M SH", "int32"))
+SCRATCH.update(_s([128, 1024], "EQ", "bfloat16"))
+SCRATCH.update(_s([128, 4096], "XG GD OV E", "bfloat16"))
+SCRATCH.update(_s([128, 4096], "GN", "float16"))
+SCRATCH.update(_s([128, 256], "A16 N16", "uint16"))
+SCRATCH.update(_s([128, 256], "AC0 AC1 TA NF0 NF1 CD CN NH MC G1 G2 G3 VR OF", "float16"))
+SCRATCH.update(_s([128, 256], "LJ HT H COND WM CW HH Y1 Y2 UP YT BIAS RST CP CN2 CQ", "bfloat16"))
+SCRATCH.update(_s([128, 256], "PM NN UU UC SB2 LAND3 YM BI CM", "float32"))
+SCRATCH.update(_s([128, 256], "EV IX ME S1 S2 SB0 SB1 LAND1 LAND2", "int32"))
+SCRATCH.update(_s([128, 128], "ROWC ROWG ID NID ID8 NID16 IDQ IDM IDW BLK NBLK BLKQ ONES", "bfloat16"))
+SCRATCH.update(_s([128, 16, 128], "SEL ONE LT", "bfloat16"))
+SCRATCH.update(_s([128, 512], "b0 b1 b2 b3 b4 b5 b6 b7", "float32", "psum"))
+DMAS = ["jt", "jm", "lm", "xw", "sd", "rt", "pk", "oq", "o3", "ox"]
+SEMAPHORES = ["sv", "sa", "st", "sg"] + ["d" + d for d in DMAS] + ["ar0", "ar1", "ar2", "lc0", "lc1", "lc2"]
+PSUM = ("b0", "b1", "b2", "b3", "b4", "b5", "b6", "b7")
+
+
+def rank_program(g, core, T, topo):
+    rank = T.rank_of(core)
+    if rank is None:
+        return
+    nxt = T.cores[(rank + 1) % len(T.cores)]
+    prv = T.cores[(rank - 1) % len(T.cores)]
+    queue = {"v": g.vector, "a": g.scalar, "t": g.tensor, "g": g, "s": g.sync}
+    count = {"sv": 0, "sa": 0, "st": 0, "sg": 0}
+    seen, wrote, readers = {}, {}, {}
+
+    def emit(q, fn, R, W, sem=None, inc=1, total=None):
+        need = {}
+
+        def want(s, v):
+            if s == "st" and q == "t":
+                return
+            if need.get(s, 0) < v:
+                need[s] = v
+        own = "s" + q
+        for tag in R:
+            if tag in wrote:
+                want(*wrote[tag])
+            if tag in PSUM:
+                for s, v in readers.get(tag, {}).items():
+                    if s != own:
+                        want(s, v)
+        for tag in W:
+            if tag in wrote:
+                want(*wrote[tag])
+            for s, v in readers.get(tag, {}).items():
+                want(s, v)
+        for s in sorted(need):
+            if seen.get((q, s), 0) < need[s]:
+                queue[q].wait_ge(T.sem[s], need[s])
+                seen[(q, s)] = need[s]
+        ins = fn()
+        if sem is None:
+            sem = own
+            count[sem] += 1
+            total = count[sem]
+        if inc:
+            ins.then_inc(T.sem[sem], inc)
+        for tag in R:
+            readers.setdefault(tag, {})[sem] = total
+        for tag in W:
+            wrote[tag] = (sem, total)
+            readers[tag] = {}
+
+    def V(R, W, fn):
+        emit("v", fn, R.split(), W.split())
+
+    def G(W, fn):
+        emit("g", fn, [], W.split())
+
+    def D(q, name, R, W, out, in_):
+        emit(q, lambda: queue[q].dma_start(out=out, in_=in_), R.split(), W.split(), "d" + name, 16, 16)
+
+    def act(R, W, out, in_, func=AF.Copy, **kw):
+        emit("a", lambda: g.scalar.activation(out=out, in_=in_, func=func, **kw), R.split(), W.split())
+
+    def mm(R, W, out, lhsT, rhs, start, stop):
+        emit("t", lambda: g.tensor.matmul(out=out, lhsT=lhsT, rhs=rhs, start=start, stop=stop), R.split(), W.split())
+
+    def cp(R, W, out, in_):
+        V(R, W, lambda: g.vector.tensor_copy(out=out, in_=in_))
+
+    def tt(R, W, out, in0, in1, op):
+        V(R, W, lambda: g.vector.tensor_tensor(out=out, in0=in0, in1=in1, op=op))
+
+    def ts(R, W, out, in0, s1, op0, s2=None, op1=None):
+        if op1 is None:
+            V(R, W, lambda: g.vector.tensor_scalar(out=out, in0=in0, scalar1=s1, scalar2=None, op0=op0))
+        else:
+            V(R, W, lambda: g.vector.tensor_scalar(out=out, in0=in0, scalar1=s1, scalar2=s2, op0=op0, op1=op1))
+
+    def fill(W, ap, c):
+        V("", W, lambda: g.vector.memset(ap, c))
+
+    def lo(b):
+        return b[:, 0:256]
+
+    def hi(b):
+        return b[:, 256:512]
+
+    D("s", "jt", "", "JT", T.JT[:], T.jt[:])
+    D("a", "jm", "", "JM", T.JM[:], T.jm[:])
+    D("s", "sd", "", "SD", T.SD[:], T.sd[:])
+    D("a", "lm", "", "LM", T.LM[:], T.lm[:])
+    D("a", "xw", "", "X", T.X[:, 0:3072], T.xw[:])
+    D("s", "pk", "", "PK", T.PK[:], T.pk[:])
+    D("s", "rt", "", "RT", T.RT[:, 0:3], T.rt[:])
+    G("PI", lambda: g.iota(T.PI[:], [[0, 16]], 0, 1))
+    G("KI", lambda: g.iota(T.KI[:], [[1, 16]], 0, 0))
+    G("ROWC", lambda: g.iota(T.ROWC[:], [[1, 128]], 0, 0, allow_small_or_imprecise_dtypes=True))
+    G("ROWG", lambda: g.iota(T.ROWG[:], [[16, 8], [0, 16]], 0, 0, allow_small_or_imprecise_dtypes=True))
+    G("ROW8", lambda: g.iota(T.ROW8[:], [[16, 8]], 0, 0, allow_small_or_imprecise_dtypes=True))
+    G("BI", lambda: g.iota(T.BI[:], [[0, 16], [-1, 16]], 15, 0, allow_small_or_imprecise_dtypes=True))
+    G("CM", lambda: g.iota(T.CM[:], [[1, 256]], 1408, 0, allow_small_or_imprecise_dtypes=True))
+    fill("CN2", T.CN2[:], -1664.0)
+    fill("HB", T.HB[:], -0.5)
+    fill("ONES", T.ONES[:], 1.0)
+    ts("PI", "PG", T.PG[:], T.PI[:], 112, OP.bitwise_and)
+    ts("PI", "PQ", T.PQ[:], T.PI[:], 15, OP.bitwise_and)
+    cp("PI", "PF", T.PF[:], T.PI[:])
+    tt("PG KI", "CK", T.CK[:], T.PG[:], T.KI[:], OP.add)
+    tt("PQ KI", "KM", T.KM[:], T.PQ[:], T.KI[:], OP.is_equal)
+    ts("ROWC PF", "ID", T.ID[:], T.ROWC[:], T.PF[:, 0:1], OP.is_equal)
+    for k in range(16):
+        ts("ID KM", "SEL", T.SEL[:, k, :], T.ID[:], T.KM[:, k:k + 1], OP.mult)
+
+    def gather_jobs(t):
+        J = "J%d" % (t % 2)
+        ac, nf = "AC%d" % (t % 2), "NF%d" % (t % 2)
+        cp("TT " + J, "A16", T.A16[:], T.TT[:].indirect(T[J][:]))
+        if t == 0:
+            ts("JT", "NT", T.NT[:], T.JT[:], 12, OP.logical_shift_right)
+        cp("NT " + J, "N16", T.N16[:], T.NT[:].indirect(T[J][:]))
+        act("LM " + J, "LJ", T.LJ[:], T.LM[:].indirect(T[J][:]))
+        ts("A16", "TA", T.TA[:], T.A16[:], -1.0, OP.mult, 1408.0, OP.add)
+        ts("A16", ac, T[ac][:], T.A16[:], -1664.0, OP.add)
+        cp("N16", nf, T[nf][:], T.N16[:])
+
+    def gather_d(c):
+        w = slice(1024 * c, 1024 * c + 1024)
+        s = slice(64 * c, 64 * c + 64)
+        act("SD A16", "GD%d" % c, T.GD[:, w], T.SD[:].indirect(T.A16[:, s]))
+        for k in range(16):
+            mm("GD%d SEL" % c, "b3", T.b3[:, s], T.SEL[:, k, :], T.GD[:, w.start + k:w.stop:16], k == 0, False)
+        mm("ID CN2", "b3", T.b3[:, s], T.ID[:], T.CN2[:, s], False, True)
+
+    def gather_n(c, t):
+        nf = "NF%d" % (t % 2)
+        w = slice(1024 * c, 1024 * c + 1024)
+        s = slice(64 * c, 64 * c + 64)
+        cp("NT N16", "GN%d" % c, T.GN[:, w], T.NT[:].indirect(T.N16[:, s]))
+        o = T.b3[:, 256 + 64 * c:320 + 64 * c]
+        for k in range(16):
+            mm("GN%d SEL" % c, "b3", o, T.SEL[:, k, :], T.GN[:, w.start + k:w.stop:16], k == 0, False)
+        mm("NID " + nf, "b3", o, T.NID[:], T[nf][:, s], False, True)
+
+    def gather_x(c, t):
+        w = slice(1024 * c, 1024 * c + 1024)
+        s = slice(64 * c, 64 * c + 64)
+        if c in XV[t]:
+            cp("X A16", "XG%d" % c, T.XG[:, w], T.X[:, 0:3072].indirect(T.A16[:, s]))
+        else:
+            act("X A16", "XG%d" % c, T.XG[:, w], T.X[:, 0:3072].indirect(T.A16[:, s]))
+
+    def sums(h):
+        for k in range(16):
+            mm("XG%d XG%d IB" % (2 * h, 2 * h + 1), "b4", T.b4[:, 128 * h + k:128 * h + 128:16], T.XG[:, 2048 * h + k:2048 * h + 2048:16],
+               T.IB[:], False, h == 1 and k == 15)
+
+    cp("JM", "J0", T.J0[:], T.JM[:])
+    ts("JT", "TT", T.TT[:], T.JT[:], 4095, OP.bitwise_and)
+    gather_jobs(0)
+    ts("ID", "NID", T.NID[:], T.ID[:], -1.0, OP.mult)
+    for c in range(4):
+        gather_d(c)
+        gather_n(c, 0)
+    ts("ROW8 CK", "IB", T.IB[:], T.ROW8[:], T.CK[:, 0:1], OP.is_equal, 16.0, OP.mult)
+    ts("BI", "BIAS", T.BIAS[:], T.BI[:], 1.0 / 128, OP.mult)
+
+    def constants():
+        for k in range(16):
+            ts("ROWC CK", "ONE", T.ONE[:, k, :], T.ROWC[:], T.CK[:, k:k + 1], OP.is_equal)
+        fill("RST", T.RST[:], 1.0)
+        fill("RST", T.RST[:, 0::16], 0.0)
+        fill("CP", T.CP[:], 1664.0)
+        fill("CQ", T.CQ[:], -2048.0)
+        fill("EB", T.EB[:], -8.0)
+        for i, x in enumerate((12288.0, 8192.0, 4096.0, -1664.0, BIG)):
+            fill("BB", T.BB[:, i:i + 1], x)
+        for nm, f in (("ID8", 8.0), ("NID16", -16.0), ("IDQ", 16384.0), ("IDM", -1408.0), ("IDW", 3072.0)):
+            ts("ID", nm, T[nm][:], T.ID[:], f, OP.mult)
+        ts("ROWG CK", "BLK", T.BLK[:], T.ROWG[:], T.CK[:, 0:1], OP.is_equal)
+        ts("BLK", "NBLK", T.NBLK[:], T.BLK[:], -1.0, OP.mult)
+        ts("BLK", "BLKQ", T.BLKQ[:], T.BLK[:], 4096.0, OP.mult)
+        tt("PQ KI", "LTM", T.LTM[:], T.PQ[:], T.KI[:], OP.is_lt)
+        ts("PQ", "THR", T.THR[:], T.PQ[:, 0:1], KD[0] - 0.5, OP.is_ge, 8.0, OP.mult)
+        cp("RT", "RTF", T.RTF[:, 0:3], T.RT[:, 0:3])
+        for r in range(1, 16):
+            ts("BLK LTM", "LT", T.LT[:, r, :], T.BLK[:], T.LTM[:, r:r + 1], OP.mult, 4096.0, OP.mult)
+
+    def heavy():
+        V("RST b4", "PM", lambda: g.vector.tensor_tensor_scan(out=T.PM[:], data0=T.RST[:], data1=lo(T.b4), initial=0.0, op0=OP.mult, op1=OP.max))
+        cp("PM", "PM", T.PM[:, 7::16], T.PM[:, 15::16])
+        cp("PM", "PM", T.PM[:, 3::8], T.PM[:, 7::8])
+        cp("PM", "PM", T.PM[:, 1::4], T.PM[:, 3::4])
+        cp("PM", "PM", T.PM[:, 0::2], T.PM[:, 1::2])
+        tt("b4 PM", "HT", T.HT[:], lo(T.b4), T.PM[:], OP.is_equal)
+
+    def over_a(i):
+        xg = "XG0 XG1 XG2 XG3"
+        b = "b%d" % (i % 2)
+        k0, k1 = KA[2 * i], KA[2 * i + 1]
+        mm(xg + " ID", b, lo(T[b]), T.ID[:], T.XG[:, k0::16], True, False)
+        mm("NID LJ", b, lo(T[b]), T.NID[:], T.LJ[:], False, True)
+        mm(xg + " ID", b, hi(T[b]), T.ID[:], T.XG[:, k1::16], True, False)
+        mm("NID LJ", b, hi(T[b]), T.NID[:], T.LJ[:], False, True)
+        act(b + " HB", "OVA%d OVA%d" % (k0, k1), T.OV[:, 256 * k0:256 * k0 + 512], T[b][:], AF.Sign, bias=T.HB[:])
+
+    def over_v(k):
+        tt("XG0 XG1 XG2 XG3 b7", "OVD%d" % k, T.OV[:, 256 * k:256 * k + 256], T.XG[:, k::16], lo(T.b7), OP.is_gt)
+
+    def wear(t, fillers):
+        mm("ONES BIAS", "b4", lo(T.b4), T.ONES[:], T.BIAS[:], True, False)
+        for c in range(4):
+            if c not in XV[t]:
+                gather_x(c, t)
+        fillers()
+        for c in XV[t]:
+            gather_x(c, t)
+        mm("ID LJ", "b7", lo(T.b7), T.ID[:], T.LJ[:], True, True)
+        sums(0)
+        over_a(0) if 0 else None
+        sums(1)
+        for i in range(len(KA) // 2):
+            over_a(i)
+        heavy()
+        for k in KD:
+            over_v(k)
+        for h in range(2):
+            mm("HT ID", "b5", T.b5[:, 128 * h:128 * h + 128], T.HT[:, 128 * h:128 * h + 128], T.ID[:], True, True)
+        act("b5", "H", T.H[:], lo(T.b5))
+        ks = [k for i in range(16) for k in (KA[i:i + 1] + KD[i:i + 1])]
+        for i, k in enumerate(ks):
+            mm(("OVA%d" if k in KA else "OVD%d") % k + " ONE", "b2", lo(T.b2), T.ONE[:, k, :], T.OV[:, 256 * k:256 * k + 256], i == 0, i == 15)
+
+    def list_of(R, src, o):
+        for r in range(16):
+            mm(R + " ONE", "b7", T.b7[:, o:o + 16], T.ONE[:, r, :], src[:, r::16], r == 0, r == 15)
+
+    def pocket3(t):
+        return ("Q3", T.Q[:, 768:1024]) if t == 0 else ("LAND%d" % t, T["LAND%d" % t][:])
+
+    def victims(t):
+        q3, l3 = pocket3(t)
+        tt("Q0 Q1", "b5", hi(T.b5), T.Q[:, 0:256], T.Q[:, 256:512], OP.max)
+        tt("b5 Q2", "b5", hi(T.b5), T.Q[:, 512:768], hi(T.b5), OP.max)
+        tt("b5 " + q3, "EV", T.EV[:], l3, hi(T.b5), OP.max)
+        ts("EV", "ME", T.ME[:], T.EV[:], 4095, OP.bitwise_and)
+        ts("EV", "IX", T.IX[:], T.EV[:], 12, OP.logical_shift_right, 3, OP.bitwise_and)
+        for i in range(3):
+            ts("IX", "GI%d" % i, T.GI[:, 256 * i:256 * i + 256], T.IX[:], float(3 - i), OP.is_equal)
+        ts("ME", "MC", T.MC[:], T.ME[:], -1664.0, OP.add)
+        if t:
+            ts(q3, "M3", T.M[:, 768:1024], l3, 4095, OP.bitwise_and)
+
+    def init_pockets():
+        ts("PK", "SH", T.SH[:], T.PK[:], 12, OP.logical_shift_right)
+        ts("PK", "M0 M1 M2 M3", T.M[:], T.PK[:], 4095, OP.bitwise_and)
+        for i in range(4):
+            s = slice(256 * i, 256 * i + 256)
+            b = "b6" if i % 2 else "b5"
+            ts("SH", b, hi(T[b]), T.SH[:, s], 12288.0, OP.mult, 4096.0 * (3 - i), OP.add)
+            tt("PK " + b, "Q%d" % i, T.Q[:, s], T.PK[:, s], hi(T[b]), OP.add)
+
+    def finish_pockets():
+        ts("Q0 Q1 Q2", "SH", T.SH[:, 0:768], T.Q[:, 0:768], 14, OP.logical_shift_right)
+        for i in range(3):
+            s = slice(256 * i, 256 * i + 256)
+            b = ("b0", "b1", "b2")[i]
+            ts("SH", b, lo(T[b]), T.SH[:, s], -12288.0, OP.mult, -4096.0 * (3 - i), OP.add)
+            tt("Q%d " % i + b, "OUTP%d" % i, T.OUTP[:, s], T.Q[:, s], lo(T[b]), OP.add)
+        D("s", "oq", "OUTP0 OUTP1 OUTP2", "YP", T.yp[:, 0:768], T.OUTP[:])
+
+    def sel(i):
+        s = slice(256 * i, 256 * i + 256)
+        eq = [T.EQ[:, 256 * j:256 * j + 256] for j in range(4)]
+        b, o = (("b6", lo(T.b6)), ("b6", hi(T.b6)), ("b1", hi(T.b1)))[i]
+        mm("ID8 EQ%d" % i, b, o, T.ID8[:], eq[i], True, False)
+        for j in range(4):
+            if j < i:
+                mm("NID16 EQ%d" % j, b, o, T.NID16[:], eq[j], False, False)
+            elif j > i:
+                mm("NID EQ%d" % j, b, o, T.NID[:], eq[j], False, False)
+        mm("ID GI%d" % i, b, o, T.ID[:], T.GI[:, s], False, True)
+        ts(b, "SL%d" % i, T.SL[:, s], o, 0.5, OP.is_ge)
+
+    def update(i, t):
+        s = slice(256 * i, 256 * i + 256)
+        b, o = (("b0", lo(T.b0)), ("b0", hi(T.b0)), ("b1", lo(T.b1)))[i]
+        tt("Q%d " % i + b, b, o, o, T.Q[:, s], OP.subtract)
+        tt("SL%d " % i + b, b, o, T.SL[:, s], o, OP.mult)
+        tt("Q%d " % i + b, "Q%d" % i, T.Q[:, s], T.Q[:, s], o, OP.add)
+        if t < 2:
+            ts("Q%d" % i, "M%d" % i, T.M[:, s], T.Q[:, s], 4095, OP.bitwise_and)
+
+    def wrap():
+        tt("TA b3", "WM", T.WM[:], T.TA[:], lo(T.b3), OP.is_gt)
+
+    def first_fill():
+        wrap()
+        constants()
+        init_pockets()
+        victims(0)
+    wear(0, first_fill)
+
+    for t in range(3):
+        last = t == 2
+        J, J2 = "J%d" % (t % 2), "J%d" % ((t + 1) % 2)
+        ac, nf = "AC%d" % (t % 2), "NF%d" % (t % 2)
+
+        def tool(b, o, first, stop):
+            mm("ID " + ac, b, o, T.ID[:], T[ac][:], first, False)
+            mm("ID CP", b, o, T.ID[:], T.CP[:], False, False)
+            mm("IDM COND", b, o, T.IDM[:], T.COND[:], False, False)
+            mm("ID CD", b, o, T.ID[:], T.CD[:], False, False)
+            mm("IDW CW", b, o, T.IDW[:], T.CW[:], False, stop)
+        ts("b2 THR", "COND", T.COND[:], lo(T.b2), T.THR[:], OP.is_gt)
+        tt("COND b3", "CN", T.CN[:], T.COND[:], hi(T.b3), OP.mult)
+        mm("ID " + nf, "b6", hi(T.b6), T.ID[:], T[nf][:], True, False)
+        mm("ID CN", "b6", hi(T.b6), T.ID[:], T.CN[:], False, True)
+        act("b6", "NN", T.NN[:], hi(T.b6))
+        tt("COND b3", "CD", T.CD[:], T.COND[:], lo(T.b3), OP.mult)
+        tt("COND WM", "CW", T.CW[:], T.COND[:], T.WM[:], OP.mult)
+        tool("b6", lo(T.b6), True, True)
+        if not last:
+            tt("NN b5", "NH", T.NH[:], T.NN[:], lo(T.b5), OP.mult)
+        tt("MC b5", "G1", T.G1[:], T.MC[:], lo(T.b5), OP.mult)
+        for i in range(4):
+            tt("M%d b6" % i, "EQ%d" % i, T.EQ[:, 256 * i:256 * i + 256], T.M[:, 256 * i:256 * i + 256], lo(T.b6), OP.is_equal)
+        act("b6 BB", "UC", T.UC[:], lo(T.b6), AF.Identity, bias=T.BB[:, 3:4])
+        if not last:
+            act("b6", "UU", T.UU[:], lo(T.b6))
+            list_of("NH", T.NH, 288)
+        for i in range(4):
+            mm("ID EQ%d" % i, "b2", hi(T.b2), T.ID[:], T.EQ[:, 256 * i:256 * i + 256], i == 0, i == 3)
+        if not last:
+            cp("b7", J2, T[J2][:], T.b7[:, 288:304])
+        tt("H b2", "b5", hi(T.b5), T.H[:], hi(T.b2), OP.min)
+        act("b5", "HH", T.HH[:], hi(T.b5))
+        act("b2 BB", "b2", lo(T.b2), hi(T.b2), AF.Relu, scale=-BIG, bias=T.BB[:, 4:5])
+        tt("UC b5", "G2", T.G2[:], T.UC[:], hi(T.b5), OP.mult)
+        tt("MC b5", "G3", T.G3[:], T.MC[:], hi(T.b5), OP.mult)
+        mm("BLK G1", "b7", lo(T.b7), T.BLK[:], T.G1[:], True, False)
+        mm("BLK G2", "b7", lo(T.b7), T.BLK[:], T.G2[:], False, False)
+        mm("NBLK G3", "b7", lo(T.b7), T.NBLK[:], T.G3[:], False, True)
+
+        def give():
+            q3, l3 = pocket3(t)
+            tt(q3 + " b2", "b2", lo(T.b2), l3, lo(T.b2), OP.max)
+            tt("EV b2", "S1", T.S1[:], T.EV[:], lo(T.b2), OP.min)
+            sb = "SB%d" % t
+            if not last:
+                ts("S1", sb, T[sb][:], T.S1[:], 0xFFCFFF, OP.bitwise_and)
+            else:
+                ts("S1", "S2", T.S2[:], T.S1[:], 0xFFCFFF, OP.bitwise_and)
+                ts("S1", "IX", T.IX[:], T.S1[:], 14, OP.logical_shift_right)
+                ts("IX", "b2", lo(T.b2), T.IX[:], -12288.0, OP.mult)
+                tt("S2 b2", sb, T[sb][:], T.S2[:], lo(T.b2), OP.add)
+            rid, pid = topo.addr(nxt)[0:2]
+            emit("g", lambda: g.remote_dma(out_ap=T["LAND%d" % (t + 1)][:], in_ap=T[sb][:], remote_sem=T.sem["ar%d" % t], local_sem=T.sem["lc%d" % t],
+                                           pid=pid, routing_id=rid, dma_engine_mask=topo.mask(core, nxt)),
+                 [sb], [], "lc%d" % t, 0, len(topo.engines(core, nxt)))
+            wrote["LAND%d" % (t + 1)] = ("ar%d" % t, len(topo.engines(prv, core)))
+        if not last:
+            cp("UU " + J, "TT", T.TT[:].indirect(T[J][:]), T.UU[:])
+        else:
+            give()
+        cp("b7", "VR", T.VR[:], lo(T.b7))
+        list_of("VR", T.VR, 256)
+        if not last:
+            cp("NN " + J, "NT", T.NT[:].indirect(T[J][:]), T.NN[:])
+            gather_jobs(t + 1)
+        mm("BLK HH", "b2", hi(T.b2), T.BLK[:], T.HH[:], True, True)
+        act("b2", "UP", T.UP[:], hi(T.b2))
+        if not last:
+            gather_d(0)
+        ts("b7", "VL", T.VL[:], T.b7[:, 256:272], 0.0625, OP.mult, 1664.0, OP.add)
+        ts("b7", "VLF", T.VLF[:], T.b7[:, 256:272], 0.0625, OP.mult)
+        for q in range(16):
+            ts("VR VLF", "E%d" % q, T.E[:, 256 * q + 16 * q:256 * q + 256], T.VR[:, 16 * q:256], T.VLF[:, q:q + 1], OP.is_equal)
+        act("X VL EB", "Y2", T.Y2[:], T.X[:, 0:3072].indirect(T.VL[:]), AF.Relu, bias=T.EB[:])
+        mm("ID CQ", "b5", lo(T.b5), T.ID[:], T.CQ[:], True, False)
+        for q in range(15):
+            mm("BLKQ E%d" % q, "b5", T.b5[:, 16 * q + 16:256], T.BLKQ[:], T.E[:, 256 * q + 16 * q + 16:256 * q + 256], False, False)
+        ee = " ".join("E%d" % q for q in range(16))
+        for r in range(1, 16):
+            mm("LT " + ee, "b5", T.b5[:, r:256:16], T.LT[:, r, :], T.E[:, r::272], False, r == 15)
+        ts("X VL RTF", "Y1", T.Y1[:], T.X[:, 0:3072].indirect(T.VL[:]), T.RTF[:, t:t + 1], OP.add, 255.0, OP.min)
+        if not last:
+            give()
+        tt("CM b5", "YM", T.YM[:], T.CM[:], lo(T.b5), OP.min)
+        tt("YM b7", "OF", T.OF[:], T.YM[:], lo(T.b7), OP.max)
+        list_of("OF", T.OF, 272)
+        mm("ID Y1", "b5", hi(T.b5), T.ID[:], T.Y1[:], True, False)
+        mm("NID Y2", "b5", hi(T.b5), T.NID[:], T.Y2[:], False, True)
+        mm("IDQ " + nf, "b1", hi(T.b1), T.IDQ[:], T[nf][:], True, False)
+        mm("IDQ CN", "b1", hi(T.b1), T.IDQ[:], T.CN[:], False, False)
+        tool("b1", hi(T.b1), False, True)
+        if not last:
+            gather_d(1)
+        for i in range(3):
+            b, o = (("b0", lo(T.b0)), ("b0", hi(T.b0)), ("b1", lo(T.b1)))[i]
+            act("b1 BB", b, o, hi(T.b1), AF.Identity, bias=T.BB[:, i:i + 1])
+        tt("UP b5", "YT", T.YT[:], T.UP[:], hi(T.b5), OP.mult)
+        if not last:
+            sel(0)
+        ts("b7", "OL", T.OL[:], T.b7[:, 272:288], 0.0625, OP.mult, 1664.0, OP.add)
+        V("Y2 YT OL", "X", lambda: g.vector.tensor_tensor(out=T.X[:].indirect(T.OL[:]), in0=T.Y2[:], in1=T.YT[:], op=OP.add))
+        if last:
+            D("s", "ox", "X", "YX", T.yx[:, 0:3072], T.X[:, 0:3072])
+            for i in range(3):
+                sel(i)
+            for i in range(3):
+                update(i, t)
+            finish_pockets()
+            D("a", "o3", "LAND3", "YP3", T.yp[:, 768:1024], T.LAND3[:])
+        else:
+            gather_d(2)
+            gather_d(3)
+
+            def fillers():
+                for c in range(2):
+                    gather_n(c, t + 1)
+                for i in range(1, 3):
+                    sel(i)
+                for i in range(3):
+                    update(i, t)
+                wrap()
+                for c in range(2, 4):
+                    gather_n(c, t + 1)
+                victims(t + 1)
+            wear(t + 1, fillers)
+    for s in ("sv", "sa", "st", "sg"):
+        g.wait_ge(T.sem[s], count[s])
+    for d in DMAS:
+        g.wait_ge(T.sem["d" + d], 16)
+    for t in range(3):
+        g.wait_ge(T.sem["lc%d" % t], len(topo.engines(core, nxt)))
+        g.wait_ge(T.sem["ar%d" % t], len(topo.engines(prv, core)))

@@ -2,9 +2,10 @@ from concourse.mybir import AluOpType, ActivationFunctionType
 
 OP = AluOpType
 AF = ActivationFunctionType
-KD = (8, 9, 10, 11, 12, 13, 14, 15)
-KA = tuple(k for k in range(16) if k not in KD)
-XV = ((2, 3), (3,), (3,))
+KDS = (12, 10, 10)
+XV = ((2, 3), (), ())
+FL = (3, 4)
+NB = 3
 BIG = 16777216.0
 
 
@@ -19,23 +20,23 @@ SCRATCH.update(_s([128, 768], "JT TT NT", "int32"))
 SCRATCH.update(_s([128, 768], "LM GI SL", "bfloat16"))
 SCRATCH.update(_s([128, 768], "OUTP", "float32"))
 SCRATCH.update(_s([128, 4], "RT", "bfloat16"))
-SCRATCH.update(_s([128, 4], "RTF", "float32"))
+SCRATCH.update(_s([128, 4], "RTF THR", "float32"))
 SCRATCH.update(_s([128, 8], "BB", "float32"))
 SCRATCH.update(_s([128, 8], "ROW8 IB", "bfloat16"))
-SCRATCH.update(_s([128, 1], "THR HB EB", "float32"))
+SCRATCH.update(_s([128, 1], "HB EB", "float32"))
 SCRATCH.update(_s([128, 16], "JM PI KI PG PQ", "int32"))
 SCRATCH.update(_s([128, 16], "J0 J1 VL OL", "uint16"))
-SCRATCH.update(_s([128, 16], "VLF PF CK KM LTM", "float32"))
+SCRATCH.update(_s([128, 16], "VLF PF CK KM", "float32"))
 SCRATCH.update(_s([128, 1024], "PK Q M SH", "int32"))
 SCRATCH.update(_s([128, 1024], "EQ", "bfloat16"))
 SCRATCH.update(_s([128, 4096], "XG GD OV E", "bfloat16"))
 SCRATCH.update(_s([128, 4096], "GN", "float16"))
 SCRATCH.update(_s([128, 256], "A16 N16", "uint16"))
 SCRATCH.update(_s([128, 256], "AC0 AC1 TA NF0 NF1 CD CN NH MC G1 G2 G3 VR OF", "float16"))
-SCRATCH.update(_s([128, 256], "LJ HT H COND WM CW HH Y1 Y2 UP YT BIAS RST CP CN2 CQ", "bfloat16"))
-SCRATCH.update(_s([128, 256], "PM NN UU UC SB2 LAND3 YM BI CM", "float32"))
+SCRATCH.update(_s([128, 256], "LJ HT H COND CW HH Y1 Y2 UP YT C255 BIAS RST CP CN2 CQ", "bfloat16"))
+SCRATCH.update(_s([128, 256], "PM NN UU UC SB2 LAND3 YM CM", "float32"))
 SCRATCH.update(_s([128, 256], "EV IX ME S1 S2 SB0 SB1 LAND1 LAND2", "int32"))
-SCRATCH.update(_s([128, 128], "ROWC ROWG ID NID ID8 NID16 IDQ IDM IDW BLK NBLK BLKQ ONES", "bfloat16"))
+SCRATCH.update(_s([128, 128], "ROWC ID NID ID8 NID16 IDQ IDM IDW BLK NBLK BLKQ ONES", "bfloat16"))
 SCRATCH.update(_s([128, 16, 128], "SEL ONE LT", "bfloat16"))
 SCRATCH.update(_s([128, 512], "b0 b1 b2 b3 b4 b5 b6 b7", "float32", "psum"))
 DMAS = ["jt", "jm", "lm", "xw", "sd", "rt", "pk", "oq", "o3", "ox"]
@@ -94,9 +95,6 @@ def rank_program(g, core, T, topo):
     def V(R, W, fn):
         emit("v", fn, R.split(), W.split())
 
-    def G(W, fn):
-        emit("g", fn, [], W.split())
-
     def D(q, name, R, W, out, in_):
         emit(q, lambda: queue[q].dma_start(out=out, in_=in_), R.split(), W.split(), "d" + name, 16, 16)
 
@@ -130,102 +128,109 @@ def rank_program(g, core, T, topo):
     D("s", "jt", "", "JT", T.JT[:], T.jt[:])
     D("a", "jm", "", "JM", T.JM[:], T.jm[:])
     D("s", "sd", "", "SD", T.SD[:], T.sd[:])
-    D("a", "lm", "", "LM", T.LM[:], T.lm[:])
     D("a", "xw", "", "X", T.X[:, 0:3072], T.xw[:])
+    D("a", "lm", "", "LM", T.LM[:], T.lm[:])
     D("s", "pk", "", "PK", T.PK[:], T.pk[:])
     D("s", "rt", "", "RT", T.RT[:, 0:3], T.rt[:])
-    G("PI", lambda: g.iota(T.PI[:], [[0, 16]], 0, 1))
-    G("KI", lambda: g.iota(T.KI[:], [[1, 16]], 0, 0))
-    G("ROWC", lambda: g.iota(T.ROWC[:], [[1, 128]], 0, 0, allow_small_or_imprecise_dtypes=True))
-    G("ROWG", lambda: g.iota(T.ROWG[:], [[16, 8], [0, 16]], 0, 0, allow_small_or_imprecise_dtypes=True))
-    G("ROW8", lambda: g.iota(T.ROW8[:], [[16, 8]], 0, 0, allow_small_or_imprecise_dtypes=True))
-    G("BI", lambda: g.iota(T.BI[:], [[0, 16], [-1, 16]], 15, 0, allow_small_or_imprecise_dtypes=True))
-    G("CM", lambda: g.iota(T.CM[:], [[1, 256]], 1408, 0, allow_small_or_imprecise_dtypes=True))
+
+    def iota(nm, pattern, base=0, cm=0, exact=True):
+        if exact:
+            emit("g", lambda: g.iota(T[nm][:], pattern, base, cm), [], [nm])
+        else:
+            emit("g", lambda: g.iota(T[nm][:], pattern, base, cm, allow_small_or_imprecise_dtypes=True), [], [nm])
+
+    def select(nm, pattern, op, base, cm):
+        emit("g", lambda: g.affine_select(T[nm][:], T[nm][:], pattern, op, 0.0, base, cm), [nm], [nm])
+    iota("PI", [[0, 16]], 0, 1)
+    iota("KI", [[1, 16]])
+    iota("ROWC", [[1, 128]], exact=False)
+    iota("ROW8", [[16, 8]], exact=False)
+    iota("BIAS", [[0, 16], [-1, 16]], 15, exact=False)
+    iota("RST", [[0, 256]], 1, exact=False)
+    select("RST", [[0, 16], [1, 16]], OP.not_equal, 0, 0)
+    iota("CP", [[0, 256]], 1664, exact=False)
+    blocks = [[0, 16], [0, 8], [0, 16]]
+    iota("ONE", blocks, 1, exact=False)
+    select("ONE", [[-1, 16], [0, 8], [1, 16]], OP.is_equal, 0, 0)
+    select("ONE", [[0, 16], [-16, 8], [0, 16]], OP.is_ge, 0, 1)
+    select("ONE", [[0, 16], [16, 8], [0, 16]], OP.is_ge, 15, -1)
+    for nm, x in (("BLK", 1), ("NBLK", -1), ("BLKQ", 4096)):
+        iota(nm, [[0, 128]], x, exact=False)
+        select(nm, [[-16, 8], [0, 16]], OP.is_ge, 0, 1)
+        select(nm, [[16, 8], [0, 16]], OP.is_ge, 15, -1)
+    iota("LT", blocks, 4096, exact=False)
+    select("LT", [[0, 16], [-16, 8], [0, 16]], OP.is_ge, 0, 1)
+    select("LT", [[1, 16], [16, 8], [0, 16]], OP.is_ge, -1, -1)
+    iota("CQ", [[0, 256]], -2048, exact=False)
+    iota("C255", [[0, 256]], 255, exact=False)
+    iota("CM", [[1, 256]], 1408, exact=False)
     fill("CN2", T.CN2[:], -1664.0)
     fill("HB", T.HB[:], -0.5)
-    fill("ONES", T.ONES[:], 1.0)
-    ts("PI", "PG", T.PG[:], T.PI[:], 112, OP.bitwise_and)
-    ts("PI", "PQ", T.PQ[:], T.PI[:], 15, OP.bitwise_and)
+    fill("EB", T.EB[:], -8.0)
+    fill("ONES", T.ONES[:], 1.0 / 128)
+    for i, x in enumerate((12288.0, 8192.0, 4096.0, -1664.0, BIG)):
+        fill("BB", T.BB[:, i:i + 1], x)
     cp("PI", "PF", T.PF[:], T.PI[:])
-    tt("PG KI", "CK", T.CK[:], T.PG[:], T.KI[:], OP.add)
-    tt("PQ KI", "KM", T.KM[:], T.PQ[:], T.KI[:], OP.is_equal)
     ts("ROWC PF", "ID", T.ID[:], T.ROWC[:], T.PF[:, 0:1], OP.is_equal)
+    ts("PI", "PQ", T.PQ[:], T.PI[:], 15, OP.bitwise_and)
+    tt("PQ KI", "KM", T.KM[:], T.PQ[:], T.KI[:], OP.is_equal)
     for k in range(16):
         ts("ID KM", "SEL", T.SEL[:, k, :], T.ID[:], T.KM[:, k:k + 1], OP.mult)
+
+    def gather_tools(t):
+        J = "J%d" % (t % 2)
+        cp("TT " + J, "A16", T.A16[:], T.TT[:].indirect(T[J][:]))
 
     def gather_jobs(t):
         J = "J%d" % (t % 2)
         ac, nf = "AC%d" % (t % 2), "NF%d" % (t % 2)
-        cp("TT " + J, "A16", T.A16[:], T.TT[:].indirect(T[J][:]))
         if t == 0:
             ts("JT", "NT", T.NT[:], T.JT[:], 12, OP.logical_shift_right)
         cp("NT " + J, "N16", T.N16[:], T.NT[:].indirect(T[J][:]))
-        act("LM " + J, "LJ", T.LJ[:], T.LM[:].indirect(T[J][:]))
+        if t:
+            act("LM " + J, "LJ", T.LJ[:], T.LM[:].indirect(T[J][:]))
         ts("A16", "TA", T.TA[:], T.A16[:], -1.0, OP.mult, 1408.0, OP.add)
         ts("A16", ac, T[ac][:], T.A16[:], -1664.0, OP.add)
         cp("N16", nf, T[nf][:], T.N16[:])
+
+    defer, dd, held = [], [], []
+
+    def flush_d():
+        while dd:
+            dd.pop(0)()
+
+    def flush():
+        if defer:
+            defer.pop(0)()
 
     def gather_d(c):
         w = slice(1024 * c, 1024 * c + 1024)
         s = slice(64 * c, 64 * c + 64)
         act("SD A16", "GD%d" % c, T.GD[:, w], T.SD[:].indirect(T.A16[:, s]))
-        for k in range(16):
-            mm("GD%d SEL" % c, "b3", T.b3[:, s], T.SEL[:, k, :], T.GD[:, w.start + k:w.stop:16], k == 0, False)
-        mm("ID CN2", "b3", T.b3[:, s], T.ID[:], T.CN2[:, s], False, True)
+
+        def later():
+            for k in range(16):
+                mm("GD%d SEL" % c, "b3", T.b3[:, s], T.SEL[:, k, :], T.GD[:, w.start + k:w.stop:16], k == 0, False)
+            mm("ID CN2", "b3", T.b3[:, s], T.ID[:], T.CN2[:, s], False, True)
+        dd.append(later)
 
     def gather_n(c, t):
         nf = "NF%d" % (t % 2)
         w = slice(1024 * c, 1024 * c + 1024)
         s = slice(64 * c, 64 * c + 64)
         cp("NT N16", "GN%d" % c, T.GN[:, w], T.NT[:].indirect(T.N16[:, s]))
-        o = T.b3[:, 256 + 64 * c:320 + 64 * c]
-        for k in range(16):
-            mm("GN%d SEL" % c, "b3", o, T.SEL[:, k, :], T.GN[:, w.start + k:w.stop:16], k == 0, False)
-        mm("NID " + nf, "b3", o, T.NID[:], T[nf][:, s], False, True)
 
-    def gather_x(c, t):
-        w = slice(1024 * c, 1024 * c + 1024)
-        s = slice(64 * c, 64 * c + 64)
-        if c in XV[t]:
-            cp("X A16", "XG%d" % c, T.XG[:, w], T.X[:, 0:3072].indirect(T.A16[:, s]))
-        else:
-            act("X A16", "XG%d" % c, T.XG[:, w], T.X[:, 0:3072].indirect(T.A16[:, s]))
+        def later():
+            o = T.b3[:, 256 + 64 * c:320 + 64 * c]
+            for k in range(16):
+                mm("GN%d SEL" % c, "b3", o, T.SEL[:, k, :], T.GN[:, w.start + k:w.stop:16], k == 0, False)
+            mm("NID " + nf, "b3", o, T.NID[:], T[nf][:, s], False, True)
+        defer.append(later)
 
     def sums(h):
         for k in range(16):
             mm("XG%d XG%d IB" % (2 * h, 2 * h + 1), "b4", T.b4[:, 128 * h + k:128 * h + 128:16], T.XG[:, 2048 * h + k:2048 * h + 2048:16],
                T.IB[:], False, h == 1 and k == 15)
-
-    cp("JM", "J0", T.J0[:], T.JM[:])
-    ts("JT", "TT", T.TT[:], T.JT[:], 4095, OP.bitwise_and)
-    gather_jobs(0)
-    ts("ID", "NID", T.NID[:], T.ID[:], -1.0, OP.mult)
-    for c in range(4):
-        gather_d(c)
-        gather_n(c, 0)
-    ts("ROW8 CK", "IB", T.IB[:], T.ROW8[:], T.CK[:, 0:1], OP.is_equal, 16.0, OP.mult)
-    ts("BI", "BIAS", T.BIAS[:], T.BI[:], 1.0 / 128, OP.mult)
-
-    def constants():
-        for k in range(16):
-            ts("ROWC CK", "ONE", T.ONE[:, k, :], T.ROWC[:], T.CK[:, k:k + 1], OP.is_equal)
-        fill("RST", T.RST[:], 1.0)
-        fill("RST", T.RST[:, 0::16], 0.0)
-        fill("CP", T.CP[:], 1664.0)
-        fill("CQ", T.CQ[:], -2048.0)
-        fill("EB", T.EB[:], -8.0)
-        for i, x in enumerate((12288.0, 8192.0, 4096.0, -1664.0, BIG)):
-            fill("BB", T.BB[:, i:i + 1], x)
-        for nm, f in (("ID8", 8.0), ("NID16", -16.0), ("IDQ", 16384.0), ("IDM", -1408.0), ("IDW", 3072.0)):
-            ts("ID", nm, T[nm][:], T.ID[:], f, OP.mult)
-        ts("ROWG CK", "BLK", T.BLK[:], T.ROWG[:], T.CK[:, 0:1], OP.is_equal)
-        ts("BLK", "NBLK", T.NBLK[:], T.BLK[:], -1.0, OP.mult)
-        ts("BLK", "BLKQ", T.BLKQ[:], T.BLK[:], 4096.0, OP.mult)
-        tt("PQ KI", "LTM", T.LTM[:], T.PQ[:], T.KI[:], OP.is_lt)
-        ts("PQ", "THR", T.THR[:], T.PQ[:, 0:1], KD[0] - 0.5, OP.is_ge, 8.0, OP.mult)
-        cp("RT", "RTF", T.RTF[:, 0:3], T.RT[:, 0:3])
-        for r in range(1, 16):
-            ts("BLK LTM", "LT", T.LT[:, r, :], T.BLK[:], T.LTM[:, r:r + 1], OP.mult, 4096.0, OP.mult)
 
     def heavy():
         V("RST b4", "PM", lambda: g.vector.tensor_tensor_scan(out=T.PM[:], data0=T.RST[:], data1=lo(T.b4), initial=0.0, op0=OP.mult, op1=OP.max))
@@ -234,43 +239,50 @@ def rank_program(g, core, T, topo):
         cp("PM", "PM", T.PM[:, 1::4], T.PM[:, 3::4])
         cp("PM", "PM", T.PM[:, 0::2], T.PM[:, 1::2])
         tt("b4 PM", "HT", T.HT[:], lo(T.b4), T.PM[:], OP.is_equal)
-
-    def over_a(i):
-        xg = "XG0 XG1 XG2 XG3"
-        b = "b%d" % (i % 2)
-        k0, k1 = KA[2 * i], KA[2 * i + 1]
-        mm(xg + " ID", b, lo(T[b]), T.ID[:], T.XG[:, k0::16], True, False)
-        mm("NID LJ", b, lo(T[b]), T.NID[:], T.LJ[:], False, True)
-        mm(xg + " ID", b, hi(T[b]), T.ID[:], T.XG[:, k1::16], True, False)
-        mm("NID LJ", b, hi(T[b]), T.NID[:], T.LJ[:], False, True)
-        act(b + " HB", "OVA%d OVA%d" % (k0, k1), T.OV[:, 256 * k0:256 * k0 + 512], T[b][:], AF.Sign, bias=T.HB[:])
-
-    def over_v(k):
-        tt("XG0 XG1 XG2 XG3 b7", "OVD%d" % k, T.OV[:, 256 * k:256 * k + 256], T.XG[:, k::16], lo(T.b7), OP.is_gt)
-
-    def wear(t, fillers):
-        mm("ONES BIAS", "b4", lo(T.b4), T.ONES[:], T.BIAS[:], True, False)
-        for c in range(4):
-            if c not in XV[t]:
-                gather_x(c, t)
-        fillers()
-        for c in XV[t]:
-            gather_x(c, t)
-        mm("ID LJ", "b7", lo(T.b7), T.ID[:], T.LJ[:], True, True)
-        sums(0)
-        over_a(0) if 0 else None
-        sums(1)
-        for i in range(len(KA) // 2):
-            over_a(i)
-        heavy()
-        for k in KD:
-            over_v(k)
         for h in range(2):
             mm("HT ID", "b5", T.b5[:, 128 * h:128 * h + 128], T.HT[:, 128 * h:128 * h + 128], T.ID[:], True, True)
         act("b5", "H", T.H[:], lo(T.b5))
-        ks = [k for i in range(16) for k in (KA[i:i + 1] + KD[i:i + 1])]
-        for i, k in enumerate(ks):
-            mm(("OVA%d" if k in KA else "OVD%d") % k + " ONE", "b2", lo(T.b2), T.ONE[:, k, :], T.OV[:, 256 * k:256 * k + 256], i == 0, i == 15)
+
+    def over_a(i):
+        b = "b%d" % (i % 2)
+        for k, o in ((2 * i, lo(T[b])), (2 * i + 1, hi(T[b]))):
+            mm("NID LJ", b, o, T.NID[:], T.LJ[:], True, False)
+            mm("XG0 XG1 XG2 XG3 ID", b, o, T.ID[:], T.XG[:, k::16], False, True)
+        act(b + " HB", "OVA%d" % i, T.OV[:, 512 * i:512 * i + 512], T[b][:], AF.Sign, bias=T.HB[:])
+
+    def count_a(i, end):
+        for k in (2 * i, 2 * i + 1):
+            mm("OVA%d ONE" % i, "b2", lo(T.b2), T.ONE[:, k, :], T.OV[:, 256 * k:256 * k + 256], k == 0, k == end)
+
+    def wear(t, fillers):
+        kd = KDS[t]
+        for c in range(4):
+            if c not in XV[t]:
+                act("X A16", "XG%d" % c, T.XG[:, 1024 * c:1024 * c + 1024], T.X[:, 0:3072].indirect(T.A16[:, 64 * c:64 * c + 64]))
+        fillers(0)
+        mm("ONES BIAS", "b4", lo(T.b4), T.ONES[:], T.BIAS[:], True, False)
+        for c in XV[t]:
+            cp("X A16", "XG%d" % c, T.XG[:, 1024 * c:1024 * c + 1024], T.X[:, 0:3072].indirect(T.A16[:, 64 * c:64 * c + 64]))
+        sums(0)
+        sums(1)
+        mm("ID LJ", "b7", lo(T.b7), T.ID[:], T.LJ[:], True, True)
+        for i in range(kd // 2):
+            over_a(i)
+            if i:
+                count_a(i - 1, 15)
+            if i == 3:
+                heavy()
+                fillers(1)
+            if i in FL:
+                flush()
+        count_a(kd // 2 - 1, 15)
+        while defer:
+            flush()
+        for k in range(kd, 16):
+            tt("XG0 XG1 XG2 XG3 b7", "OVD%d" % k, T.OV[:, 256 * k:256 * k + 256], T.XG[:, k::16], lo(T.b7), OP.is_gt)
+        for k in range(kd, 16):
+            mm("OVD%d ONE" % k, "b2", lo(T.b2), T.ONE[:, k, :], T.OV[:, 256 * k:256 * k + 256], False, k == 15)
+        fillers(2)
 
     def list_of(R, src, o):
         for r in range(16):
@@ -297,9 +309,8 @@ def rank_program(g, core, T, topo):
         ts("PK", "M0 M1 M2 M3", T.M[:], T.PK[:], 4095, OP.bitwise_and)
         for i in range(4):
             s = slice(256 * i, 256 * i + 256)
-            b = "b6" if i % 2 else "b5"
-            ts("SH", b, hi(T[b]), T.SH[:, s], 12288.0, OP.mult, 4096.0 * (3 - i), OP.add)
-            tt("PK " + b, "Q%d" % i, T.Q[:, s], T.PK[:, s], hi(T[b]), OP.add)
+            ts("SH", "b6", hi(T.b6), T.SH[:, s], 12288.0, OP.mult, 4096.0 * (3 - i), OP.add)
+            tt("PK b6", "Q%d" % i, T.Q[:, s], T.PK[:, s], hi(T.b6), OP.add)
 
     def finish_pockets():
         ts("Q0 Q1 Q2", "SH", T.SH[:, 0:768], T.Q[:, 0:768], 14, OP.logical_shift_right)
@@ -310,10 +321,10 @@ def rank_program(g, core, T, topo):
             tt("Q%d " % i + b, "OUTP%d" % i, T.OUTP[:, s], T.Q[:, s], lo(T[b]), OP.add)
         D("s", "oq", "OUTP0 OUTP1 OUTP2", "YP", T.yp[:, 0:768], T.OUTP[:])
 
-    def sel(i):
+    def sel(i, t):
         s = slice(256 * i, 256 * i + 256)
         eq = [T.EQ[:, 256 * j:256 * j + 256] for j in range(4)]
-        b, o = (("b6", lo(T.b6)), ("b6", hi(T.b6)), ("b1", hi(T.b1)))[i]
+        b, o = (("b6", lo(T.b6)), ("b6", hi(T.b6)), ("b4", lo(T.b4)))[i]
         mm("ID8 EQ%d" % i, b, o, T.ID8[:], eq[i], True, False)
         for j in range(4):
             if j < i:
@@ -321,26 +332,56 @@ def rank_program(g, core, T, topo):
             elif j > i:
                 mm("NID EQ%d" % j, b, o, T.NID[:], eq[j], False, False)
         mm("ID GI%d" % i, b, o, T.ID[:], T.GI[:, s], False, True)
-        ts(b, "SL%d" % i, T.SL[:, s], o, 0.5, OP.is_ge)
+        if t == 2:
+            act(b, b, o, o, AF.Relu)
+            act(b, "SL%d" % i, T.SL[:, s], o, AF.Sign)
+        else:
+            held.append(lambda: ts(b, "SL%d" % i, T.SL[:, s], o, 0.5, OP.is_ge))
 
-    def update(i, t):
-        s = slice(256 * i, 256 * i + 256)
-        b, o = (("b0", lo(T.b0)), ("b0", hi(T.b0)), ("b1", lo(T.b1)))[i]
-        tt("Q%d " % i + b, b, o, o, T.Q[:, s], OP.subtract)
-        tt("SL%d " % i + b, b, o, T.SL[:, s], o, OP.mult)
-        tt("Q%d " % i + b, "Q%d" % i, T.Q[:, s], T.Q[:, s], o, OP.add)
-        if t < 2:
-            ts("Q%d" % i, "M%d" % i, T.M[:, s], T.Q[:, s], 4095, OP.bitwise_and)
+    def update(t):
+        at = (("b0", lo(T.b0)), ("b0", hi(T.b0)), ("b1", lo(T.b1)))
+        for i, (b, o) in enumerate(at):
+            tt("Q%d " % i + b, b, o, o, T.Q[:, 256 * i:256 * i + 256], OP.subtract)
+        for i, (b, o) in enumerate(at):
+            s = slice(256 * i, 256 * i + 256)
+            if held:
+                held.pop(0)()
+            tt("SL%d " % i + b, b, o, T.SL[:, s], o, OP.mult)
+            tt("Q%d " % i + b, "Q%d" % i, T.Q[:, s], T.Q[:, s], o, OP.add)
+            if t < 2:
+                ts("Q%d" % i, "M%d" % i, T.M[:, s], T.Q[:, s], 4095, OP.bitwise_and)
 
     def wrap():
-        tt("TA b3", "WM", T.WM[:], T.TA[:], lo(T.b3), OP.is_gt)
+        tt("TA b3", "b4", hi(T.b4), T.TA[:], lo(T.b3), OP.is_gt)
 
-    def first_fill():
-        wrap()
-        constants()
-        init_pockets()
-        victims(0)
-    wear(0, first_fill)
+    cp("JM", "J0", T.J0[:], T.JM[:])
+    ts("JT", "TT", T.TT[:], T.JT[:], 4095, OP.bitwise_and)
+    gather_tools(0)
+    gather_jobs(0)
+    act("ID", "NID", T.NID[:], T.ID[:], scale=-1.0)
+    for c in range(4):
+        gather_d(c)
+        flush_d()
+    act("LM J0", "LJ", T.LJ[:], T.LM[:].indirect(T.J0[:]))
+    for nm, f in (("ID8", 8.0), ("NID16", -16.0), ("IDQ", 16384.0), ("IDM", -1408.0), ("IDW", 3072.0)):
+        act("ID", nm, T[nm][:], T.ID[:], scale=f)
+
+    def first(x):
+        if x == 0:
+            for c in range(4):
+                gather_n(c, 0)
+            wrap()
+            ts("PI", "PG", T.PG[:], T.PI[:], 112, OP.bitwise_and)
+            tt("PG KI", "CK", T.CK[:], T.PG[:], T.KI[:], OP.add)
+            ts("ROW8 CK", "IB", T.IB[:], T.ROW8[:], T.CK[:, 0:1], OP.is_equal, 16.0, OP.mult)
+            ts("RT", "RTF", T.RTF[:, 0:3], T.RT[:, 0:3], -1.0, OP.mult, 255.0, OP.add)
+            for t in range(3):
+                ts("PQ", "THR", T.THR[:, t:t + 1], T.PQ[:, 0:1], KDS[t] - 0.5, OP.is_ge, 8.0, OP.mult)
+        elif x == 1:
+            init_pockets()
+        else:
+            victims(0)
+    wear(0, first)
 
     for t in range(3):
         last = t == 2
@@ -353,13 +394,13 @@ def rank_program(g, core, T, topo):
             mm("IDM COND", b, o, T.IDM[:], T.COND[:], False, False)
             mm("ID CD", b, o, T.ID[:], T.CD[:], False, False)
             mm("IDW CW", b, o, T.IDW[:], T.CW[:], False, stop)
-        ts("b2 THR", "COND", T.COND[:], lo(T.b2), T.THR[:], OP.is_gt)
+        ts("b2 THR", "COND", T.COND[:], lo(T.b2), T.THR[:, t:t + 1], OP.is_gt)
         tt("COND b3", "CN", T.CN[:], T.COND[:], hi(T.b3), OP.mult)
         mm("ID " + nf, "b6", hi(T.b6), T.ID[:], T[nf][:], True, False)
         mm("ID CN", "b6", hi(T.b6), T.ID[:], T.CN[:], False, True)
         act("b6", "NN", T.NN[:], hi(T.b6))
         tt("COND b3", "CD", T.CD[:], T.COND[:], lo(T.b3), OP.mult)
-        tt("COND WM", "CW", T.CW[:], T.COND[:], T.WM[:], OP.mult)
+        tt("COND b4", "CW", T.CW[:], T.COND[:], hi(T.b4), OP.mult)
         tool("b6", lo(T.b6), True, True)
         if not last:
             tt("NN b5", "NH", T.NH[:], T.NN[:], lo(T.b5), OP.mult)
@@ -375,13 +416,19 @@ def rank_program(g, core, T, topo):
         if not last:
             cp("b7", J2, T[J2][:], T.b7[:, 288:304])
         tt("H b2", "b5", hi(T.b5), T.H[:], hi(T.b2), OP.min)
+        tt("MC b5", "G3", T.G3[:], T.MC[:], hi(T.b5), OP.mult)
+        tt("UC b5", "G2", T.G2[:], T.UC[:], hi(T.b5), OP.mult)
         act("b5", "HH", T.HH[:], hi(T.b5))
         act("b2 BB", "b2", lo(T.b2), hi(T.b2), AF.Relu, scale=-BIG, bias=T.BB[:, 4:5])
-        tt("UC b5", "G2", T.G2[:], T.UC[:], hi(T.b5), OP.mult)
-        tt("MC b5", "G3", T.G3[:], T.MC[:], hi(T.b5), OP.mult)
         mm("BLK G1", "b7", lo(T.b7), T.BLK[:], T.G1[:], True, False)
-        mm("BLK G2", "b7", lo(T.b7), T.BLK[:], T.G2[:], False, False)
-        mm("NBLK G3", "b7", lo(T.b7), T.NBLK[:], T.G3[:], False, True)
+        mm("NBLK G3", "b7", lo(T.b7), T.NBLK[:], T.G3[:], False, False)
+        mm("BLK G2", "b7", lo(T.b7), T.BLK[:], T.G2[:], False, True)
+        mm("BLK HH", "b2", hi(T.b2), T.BLK[:], T.HH[:], True, True)
+        if not last:
+            cp("UU " + J, "TT", T.TT[:].indirect(T[J][:]), T.UU[:])
+        cp("b7", "VR", T.VR[:], lo(T.b7))
+        list_of("VR", T.VR, 256)
+        act("b2", "UP", T.UP[:], hi(T.b2))
 
         def give():
             q3, l3 = pocket3(t)
@@ -391,8 +438,8 @@ def rank_program(g, core, T, topo):
             if not last:
                 ts("S1", sb, T[sb][:], T.S1[:], 0xFFCFFF, OP.bitwise_and)
             else:
-                ts("S1", "S2", T.S2[:], T.S1[:], 0xFFCFFF, OP.bitwise_and)
                 ts("S1", "IX", T.IX[:], T.S1[:], 14, OP.logical_shift_right)
+                ts("S1", "S2", T.S2[:], T.S1[:], 0xFFCFFF, OP.bitwise_and)
                 ts("IX", "b2", lo(T.b2), T.IX[:], -12288.0, OP.mult)
                 tt("S2 b2", sb, T[sb][:], T.S2[:], lo(T.b2), OP.add)
             rid, pid = topo.addr(nxt)[0:2]
@@ -401,73 +448,69 @@ def rank_program(g, core, T, topo):
                  [sb], [], "lc%d" % t, 0, len(topo.engines(core, nxt)))
             wrote["LAND%d" % (t + 1)] = ("ar%d" % t, len(topo.engines(prv, core)))
         if not last:
-            cp("UU " + J, "TT", T.TT[:].indirect(T[J][:]), T.UU[:])
+            gather_tools(t + 1)
+            gather_d(0)
+            cp("NN " + J, "NT", T.NT[:].indirect(T[J][:]), T.NN[:])
         else:
             give()
-        cp("b7", "VR", T.VR[:], lo(T.b7))
-        list_of("VR", T.VR, 256)
-        if not last:
-            cp("NN " + J, "NT", T.NT[:].indirect(T[J][:]), T.NN[:])
-            gather_jobs(t + 1)
-        mm("BLK HH", "b2", hi(T.b2), T.BLK[:], T.HH[:], True, True)
-        act("b2", "UP", T.UP[:], hi(T.b2))
-        if not last:
-            gather_d(0)
         ts("b7", "VL", T.VL[:], T.b7[:, 256:272], 0.0625, OP.mult, 1664.0, OP.add)
         ts("b7", "VLF", T.VLF[:], T.b7[:, 256:272], 0.0625, OP.mult)
         for q in range(16):
             ts("VR VLF", "E%d" % q, T.E[:, 256 * q + 16 * q:256 * q + 256], T.VR[:, 16 * q:256], T.VLF[:, q:q + 1], OP.is_equal)
         act("X VL EB", "Y2", T.Y2[:], T.X[:, 0:3072].indirect(T.VL[:]), AF.Relu, bias=T.EB[:])
+        act("X VL RTF", "Y1", T.Y1[:], T.X[:, 0:3072].indirect(T.VL[:]), AF.Relu, scale=-1.0, bias=T.RTF[:, t:t + 1])
+        mm("IDQ " + nf, "b1", hi(T.b1), T.IDQ[:], T[nf][:], True, False)
+        mm("IDQ CN", "b1", hi(T.b1), T.IDQ[:], T.CN[:], False, False)
+        tool("b1", hi(T.b1), False, True)
         mm("ID CQ", "b5", lo(T.b5), T.ID[:], T.CQ[:], True, False)
         for q in range(15):
             mm("BLKQ E%d" % q, "b5", T.b5[:, 16 * q + 16:256], T.BLKQ[:], T.E[:, 256 * q + 16 * q + 16:256 * q + 256], False, False)
         ee = " ".join("E%d" % q for q in range(16))
         for r in range(1, 16):
             mm("LT " + ee, "b5", T.b5[:, r:256:16], T.LT[:, r, :], T.E[:, r::272], False, r == 15)
-        ts("X VL RTF", "Y1", T.Y1[:], T.X[:, 0:3072].indirect(T.VL[:]), T.RTF[:, t:t + 1], OP.add, 255.0, OP.min)
         if not last:
             give()
         tt("CM b5", "YM", T.YM[:], T.CM[:], lo(T.b5), OP.min)
         tt("YM b7", "OF", T.OF[:], T.YM[:], lo(T.b7), OP.max)
-        list_of("OF", T.OF, 272)
-        mm("ID Y1", "b5", hi(T.b5), T.ID[:], T.Y1[:], True, False)
+        mm("ID C255", "b5", hi(T.b5), T.ID[:], T.C255[:], True, False)
+        mm("NID Y1", "b5", hi(T.b5), T.NID[:], T.Y1[:], False, False)
         mm("NID Y2", "b5", hi(T.b5), T.NID[:], T.Y2[:], False, True)
-        mm("IDQ " + nf, "b1", hi(T.b1), T.IDQ[:], T[nf][:], True, False)
-        mm("IDQ CN", "b1", hi(T.b1), T.IDQ[:], T.CN[:], False, False)
-        tool("b1", hi(T.b1), False, True)
+        list_of("OF", T.OF, 272)
+        if not last:
+            gather_jobs(t + 1)
+        tt("UP b5", "YT", T.YT[:], T.UP[:], hi(T.b5), OP.mult)
         if not last:
             gather_d(1)
         for i in range(3):
             b, o = (("b0", lo(T.b0)), ("b0", hi(T.b0)), ("b1", lo(T.b1)))[i]
             act("b1 BB", b, o, hi(T.b1), AF.Identity, bias=T.BB[:, i:i + 1])
-        tt("UP b5", "YT", T.YT[:], T.UP[:], hi(T.b5), OP.mult)
-        if not last:
-            sel(0)
         ts("b7", "OL", T.OL[:], T.b7[:, 272:288], 0.0625, OP.mult, 1664.0, OP.add)
         V("Y2 YT OL", "X", lambda: g.vector.tensor_tensor(out=T.X[:].indirect(T.OL[:]), in0=T.Y2[:], in1=T.YT[:], op=OP.add))
         if last:
             D("s", "ox", "X", "YX", T.yx[:, 0:3072], T.X[:, 0:3072])
             for i in range(3):
-                sel(i)
-            for i in range(3):
-                update(i, t)
+                sel(i, t)
+            update(t)
             finish_pockets()
             D("a", "o3", "LAND3", "YP3", T.yp[:, 768:1024], T.LAND3[:])
         else:
             gather_d(2)
             gather_d(3)
 
-            def fillers():
-                for c in range(2):
-                    gather_n(c, t + 1)
-                for i in range(1, 3):
-                    sel(i)
-                for i in range(3):
-                    update(i, t)
-                wrap()
-                for c in range(2, 4):
-                    gather_n(c, t + 1)
-                victims(t + 1)
+            def fillers(x):
+                if x == 0:
+                    for i in range(3):
+                        sel(i, t)
+                    flush_d()
+                    update(t)
+                    wrap()
+                    for c in range(NB):
+                        gather_n(c, t + 1)
+                elif x == 1:
+                    for c in range(NB, 4):
+                        gather_n(c, t + 1)
+                else:
+                    victims(t + 1)
             wear(t + 1, fillers)
     for s in ("sv", "sa", "st", "sg"):
         g.wait_ge(T.sem[s], count[s])

from concourse.mybir import AluOpType, ActivationFunctionType

OP = AluOpType
AF = ActivationFunctionType
KDS = (12, 10, 10)
XV = ((2, 3), (), ())
FL = (3, 4)
NB = 3
BIG = 16777216.0


def _s(shape, names, dtype, where="sbuf"):
    return {n: (where, shape, dtype) for n in names.split()}


SCRATCH = {}
SCRATCH.update(_s([128, 3328], "X", "bfloat16"))
SCRATCH.update(_s([128, 3072], "SD", "bfloat16"))
SCRATCH.update(_s([128, 768], "JT TT NT", "int32"))
SCRATCH.update(_s([128, 768], "LM GI SL", "bfloat16"))
SCRATCH.update(_s([128, 768], "OUTP", "float32"))
SCRATCH.update(_s([128, 4], "RT", "bfloat16"))
SCRATCH.update(_s([128, 4], "RTF THR", "float32"))
SCRATCH.update(_s([128, 8], "BB", "float32"))
SCRATCH.update(_s([128, 8], "ROW8 IB", "bfloat16"))
SCRATCH.update(_s([128, 1], "HB EB", "float32"))
SCRATCH.update(_s([128, 16], "JM PI KI PG PQ", "int32"))
SCRATCH.update(_s([128, 16], "J0 J1 VL OL", "uint16"))
SCRATCH.update(_s([128, 16], "VLF PF CK KM", "float32"))
SCRATCH.update(_s([128, 1024], "PK Q M SH", "int32"))
SCRATCH.update(_s([128, 1024], "EQ", "bfloat16"))
SCRATCH.update(_s([128, 4096], "XG GD OV E", "bfloat16"))
SCRATCH.update(_s([128, 4096], "GN", "float16"))
SCRATCH.update(_s([128, 256], "A16 N16", "uint16"))
SCRATCH.update(_s([128, 256], "AC0 AC1 TA NF0 NF1 CD CN NH MC G1 G2 G3 VR OF", "float16"))
SCRATCH.update(_s([128, 256], "LJ HT H COND CW HH Y1 Y2 UP YT C255 BIAS RST CP CN2 CQ", "bfloat16"))
SCRATCH.update(_s([128, 256], "PM NN UU UC SB2 LAND3 YM CM", "float32"))
SCRATCH.update(_s([128, 256], "EV IX ME S1 S2 SB0 SB1 LAND1 LAND2", "int32"))
SCRATCH.update(_s([128, 128], "ROWC ID NID ID8 NID16 IDQ IDM IDW BLK NBLK BLKQ ONES", "bfloat16"))
SCRATCH.update(_s([128, 16, 128], "SEL ONE LT", "bfloat16"))
SCRATCH.update(_s([128, 512], "b0 b1 b2 b3 b4 b5 b6 b7", "float32", "psum"))
DMAS = ["jt", "jm", "lm", "xw", "sd", "rt", "pk", "oq", "o3", "ox"]
SEMAPHORES = ["sv", "sa", "st", "sg"] + ["d" + d for d in DMAS] + ["ar0", "ar1", "ar2", "lc0", "lc1", "lc2"]
PSUM = ("b0", "b1", "b2", "b3", "b4", "b5", "b6", "b7")


def rank_program(g, core, T, topo):
    rank = T.rank_of(core)
    if rank is None:
        return
    nxt = T.cores[(rank + 1) % len(T.cores)]
    prv = T.cores[(rank - 1) % len(T.cores)]
    queue = {"v": g.vector, "a": g.scalar, "t": g.tensor, "g": g, "s": g.sync}
    count = {"sv": 0, "sa": 0, "st": 0, "sg": 0}
    seen, wrote, readers = {}, {}, {}

    def emit(q, fn, R, W, sem=None, inc=1, total=None):
        need = {}

        def want(s, v):
            if s == "st" and q == "t":
                return
            if need.get(s, 0) < v:
                need[s] = v
        own = "s" + q
        for tag in R:
            if tag in wrote:
                want(*wrote[tag])
            if tag in PSUM:
                for s, v in readers.get(tag, {}).items():
                    if s != own:
                        want(s, v)
        for tag in W:
            if tag in wrote:
                want(*wrote[tag])
            for s, v in readers.get(tag, {}).items():
                want(s, v)
        for s in sorted(need):
            if seen.get((q, s), 0) < need[s]:
                queue[q].wait_ge(T.sem[s], need[s])
                seen[(q, s)] = need[s]
        ins = fn()
        if sem is None:
            sem = own
            count[sem] += 1
            total = count[sem]
        if inc:
            ins.then_inc(T.sem[sem], inc)
        for tag in R:
            readers.setdefault(tag, {})[sem] = total
        for tag in W:
            wrote[tag] = (sem, total)
            readers[tag] = {}

    def V(R, W, fn):
        emit("v", fn, R.split(), W.split())

    def D(q, name, R, W, out, in_):
        emit(q, lambda: queue[q].dma_start(out=out, in_=in_), R.split(), W.split(), "d" + name, 16, 16)

    def act(R, W, out, in_, func=AF.Copy, **kw):
        emit("a", lambda: g.scalar.activation(out=out, in_=in_, func=func, **kw), R.split(), W.split())

    def mm(R, W, out, lhsT, rhs, start, stop):
        emit("t", lambda: g.tensor.matmul(out=out, lhsT=lhsT, rhs=rhs, start=start, stop=stop), R.split(), W.split())

    def cp(R, W, out, in_):
        V(R, W, lambda: g.vector.tensor_copy(out=out, in_=in_))

    def tt(R, W, out, in0, in1, op):
        V(R, W, lambda: g.vector.tensor_tensor(out=out, in0=in0, in1=in1, op=op))

    def ts(R, W, out, in0, s1, op0, s2=None, op1=None):
        if op1 is None:
            V(R, W, lambda: g.vector.tensor_scalar(out=out, in0=in0, scalar1=s1, scalar2=None, op0=op0))
        else:
            V(R, W, lambda: g.vector.tensor_scalar(out=out, in0=in0, scalar1=s1, scalar2=s2, op0=op0, op1=op1))

    def fill(W, ap, c):
        V("", W, lambda: g.vector.memset(ap, c))

    def lo(b):
        return b[:, 0:256]

    def hi(b):
        return b[:, 256:512]

    D("s", "jt", "", "JT", T.JT[:], T.jt[:])
    D("a", "jm", "", "JM", T.JM[:], T.jm[:])
    D("s", "sd", "", "SD", T.SD[:], T.sd[:])
    D("a", "xw", "", "X", T.X[:, 0:3072], T.xw[:])
    D("a", "lm", "", "LM", T.LM[:], T.lm[:])
    D("s", "pk", "", "PK", T.PK[:], T.pk[:])
    D("s", "rt", "", "RT", T.RT[:, 0:3], T.rt[:])

    def iota(nm, pattern, base=0, cm=0, exact=True):
        if exact:
            emit("g", lambda: g.iota(T[nm][:], pattern, base, cm), [], [nm])
        else:
            emit("g", lambda: g.iota(T[nm][:], pattern, base, cm, allow_small_or_imprecise_dtypes=True), [], [nm])

    def select(nm, pattern, op, base, cm):
        emit("g", lambda: g.affine_select(T[nm][:], T[nm][:], pattern, op, 0.0, base, cm), [nm], [nm])
    iota("PI", [[0, 16]], 0, 1)
    iota("KI", [[1, 16]])
    iota("ROWC", [[1, 128]], exact=False)
    iota("ROW8", [[16, 8]], exact=False)
    iota("BIAS", [[0, 16], [-1, 16]], 15, exact=False)
    iota("RST", [[0, 256]], 1, exact=False)
    select("RST", [[0, 16], [1, 16]], OP.not_equal, 0, 0)
    iota("CP", [[0, 256]], 1664, exact=False)
    blocks = [[0, 16], [0, 8], [0, 16]]
    iota("ONE", blocks, 1, exact=False)
    select("ONE", [[-1, 16], [0, 8], [1, 16]], OP.is_equal, 0, 0)
    select("ONE", [[0, 16], [-16, 8], [0, 16]], OP.is_ge, 0, 1)
    select("ONE", [[0, 16], [16, 8], [0, 16]], OP.is_ge, 15, -1)
    for nm, x in (("BLK", 1), ("NBLK", -1), ("BLKQ", 4096)):
        iota(nm, [[0, 128]], x, exact=False)
        select(nm, [[-16, 8], [0, 16]], OP.is_ge, 0, 1)
        select(nm, [[16, 8], [0, 16]], OP.is_ge, 15, -1)
    iota("LT", blocks, 4096, exact=False)
    select("LT", [[0, 16], [-16, 8], [0, 16]], OP.is_ge, 0, 1)
    select("LT", [[1, 16], [16, 8], [0, 16]], OP.is_ge, -1, -1)
    iota("CQ", [[0, 256]], -2048, exact=False)
    iota("C255", [[0, 256]], 255, exact=False)
    iota("CM", [[1, 256]], 1408, exact=False)
    fill("CN2", T.CN2[:], -1664.0)
    fill("HB", T.HB[:], -0.5)
    fill("EB", T.EB[:], -8.0)
    fill("ONES", T.ONES[:], 1.0 / 128)
    for i, x in enumerate((12288.0, 8192.0, 4096.0, -1664.0, BIG)):
        fill("BB", T.BB[:, i:i + 1], x)
    cp("PI", "PF", T.PF[:], T.PI[:])
    ts("ROWC PF", "ID", T.ID[:], T.ROWC[:], T.PF[:, 0:1], OP.is_equal)
    ts("PI", "PQ", T.PQ[:], T.PI[:], 15, OP.bitwise_and)
    tt("PQ KI", "KM", T.KM[:], T.PQ[:], T.KI[:], OP.is_equal)
    for k in range(16):
        ts("ID KM", "SEL", T.SEL[:, k, :], T.ID[:], T.KM[:, k:k + 1], OP.mult)

    def gather_tools(t):
        J = "J%d" % (t % 2)
        cp("TT " + J, "A16", T.A16[:], T.TT[:].indirect(T[J][:]))

    def gather_jobs(t):
        J = "J%d" % (t % 2)
        ac, nf = "AC%d" % (t % 2), "NF%d" % (t % 2)
        if t == 0:
            ts("JT", "NT", T.NT[:], T.JT[:], 12, OP.logical_shift_right)
        cp("NT " + J, "N16", T.N16[:], T.NT[:].indirect(T[J][:]))
        if t:
            act("LM " + J, "LJ", T.LJ[:], T.LM[:].indirect(T[J][:]))
        ts("A16", "TA", T.TA[:], T.A16[:], -1.0, OP.mult, 1408.0, OP.add)
        ts("A16", ac, T[ac][:], T.A16[:], -1664.0, OP.add)
        cp("N16", nf, T[nf][:], T.N16[:])

    defer, dd, held = [], [], []

    def flush_d():
        while dd:
            dd.pop(0)()

    def flush():
        if defer:
            defer.pop(0)()

    def gather_d(c):
        w = slice(1024 * c, 1024 * c + 1024)
        s = slice(64 * c, 64 * c + 64)
        act("SD A16", "GD%d" % c, T.GD[:, w], T.SD[:].indirect(T.A16[:, s]))

        def later():
            for k in range(16):
                mm("GD%d SEL" % c, "b3", T.b3[:, s], T.SEL[:, k, :], T.GD[:, w.start + k:w.stop:16], k == 0, False)
            mm("ID CN2", "b3", T.b3[:, s], T.ID[:], T.CN2[:, s], False, True)
        dd.append(later)

    def gather_n(c, t):
        nf = "NF%d" % (t % 2)
        w = slice(1024 * c, 1024 * c + 1024)
        s = slice(64 * c, 64 * c + 64)
        cp("NT N16", "GN%d" % c, T.GN[:, w], T.NT[:].indirect(T.N16[:, s]))

        def later():
            o = T.b3[:, 256 + 64 * c:320 + 64 * c]
            for k in range(16):
                mm("GN%d SEL" % c, "b3", o, T.SEL[:, k, :], T.GN[:, w.start + k:w.stop:16], k == 0, False)
            mm("NID " + nf, "b3", o, T.NID[:], T[nf][:, s], False, True)
        defer.append(later)

    def sums(h):
        for k in range(16):
            mm("XG%d XG%d IB" % (2 * h, 2 * h + 1), "b4", T.b4[:, 128 * h + k:128 * h + 128:16], T.XG[:, 2048 * h + k:2048 * h + 2048:16],
               T.IB[:], False, h == 1 and k == 15)

    def heavy():
        V("RST b4", "PM", lambda: g.vector.tensor_tensor_scan(out=T.PM[:], data0=T.RST[:], data1=lo(T.b4), initial=0.0, op0=OP.mult, op1=OP.max))
        cp("PM", "PM", T.PM[:, 7::16], T.PM[:, 15::16])
        cp("PM", "PM", T.PM[:, 3::8], T.PM[:, 7::8])
        cp("PM", "PM", T.PM[:, 1::4], T.PM[:, 3::4])
        cp("PM", "PM", T.PM[:, 0::2], T.PM[:, 1::2])
        tt("b4 PM", "HT", T.HT[:], lo(T.b4), T.PM[:], OP.is_equal)
        for h in range(2):
            mm("HT ID", "b5", T.b5[:, 128 * h:128 * h + 128], T.HT[:, 128 * h:128 * h + 128], T.ID[:], True, True)
        act("b5", "H", T.H[:], lo(T.b5))

    def over_a(i):
        b = "b%d" % (i % 2)
        for k, o in ((2 * i, lo(T[b])), (2 * i + 1, hi(T[b]))):
            mm("NID LJ", b, o, T.NID[:], T.LJ[:], True, False)
            mm("XG0 XG1 XG2 XG3 ID", b, o, T.ID[:], T.XG[:, k::16], False, True)
        act(b + " HB", "OVA%d" % i, T.OV[:, 512 * i:512 * i + 512], T[b][:], AF.Sign, bias=T.HB[:])

    def count_a(i, end):
        for k in (2 * i, 2 * i + 1):
            mm("OVA%d ONE" % i, "b2", lo(T.b2), T.ONE[:, k, :], T.OV[:, 256 * k:256 * k + 256], k == 0, k == end)

    def wear(t, fillers):
        kd = KDS[t]
        for c in range(4):
            if c not in XV[t]:
                act("X A16", "XG%d" % c, T.XG[:, 1024 * c:1024 * c + 1024], T.X[:, 0:3072].indirect(T.A16[:, 64 * c:64 * c + 64]))
        fillers(0)
        mm("ONES BIAS", "b4", lo(T.b4), T.ONES[:], T.BIAS[:], True, False)
        for c in XV[t]:
            cp("X A16", "XG%d" % c, T.XG[:, 1024 * c:1024 * c + 1024], T.X[:, 0:3072].indirect(T.A16[:, 64 * c:64 * c + 64]))
        sums(0)
        sums(1)
        mm("ID LJ", "b7", lo(T.b7), T.ID[:], T.LJ[:], True, True)
        for i in range(kd // 2):
            over_a(i)
            if i:
                count_a(i - 1, 15)
            if i == 3:
                heavy()
                fillers(1)
            if i in FL:
                flush()
        count_a(kd // 2 - 1, 15)
        while defer:
            flush()
        for k in range(kd, 16):
            tt("XG0 XG1 XG2 XG3 b7", "OVD%d" % k, T.OV[:, 256 * k:256 * k + 256], T.XG[:, k::16], lo(T.b7), OP.is_gt)
        for k in range(kd, 16):
            mm("OVD%d ONE" % k, "b2", lo(T.b2), T.ONE[:, k, :], T.OV[:, 256 * k:256 * k + 256], False, k == 15)
        fillers(2)

    def list_of(R, src, o):
        for r in range(16):
            mm(R + " ONE", "b7", T.b7[:, o:o + 16], T.ONE[:, r, :], src[:, r::16], r == 0, r == 15)

    def pocket3(t):
        return ("Q3", T.Q[:, 768:1024]) if t == 0 else ("LAND%d" % t, T["LAND%d" % t][:])

    def victims(t):
        q3, l3 = pocket3(t)
        tt("Q0 Q1", "b5", hi(T.b5), T.Q[:, 0:256], T.Q[:, 256:512], OP.max)
        tt("b5 Q2", "b5", hi(T.b5), T.Q[:, 512:768], hi(T.b5), OP.max)
        tt("b5 " + q3, "EV", T.EV[:], l3, hi(T.b5), OP.max)
        ts("EV", "ME", T.ME[:], T.EV[:], 4095, OP.bitwise_and)
        ts("EV", "IX", T.IX[:], T.EV[:], 12, OP.logical_shift_right, 3, OP.bitwise_and)
        for i in range(3):
            ts("IX", "GI%d" % i, T.GI[:, 256 * i:256 * i + 256], T.IX[:], float(3 - i), OP.is_equal)
        ts("ME", "MC", T.MC[:], T.ME[:], -1664.0, OP.add)
        if t:
            ts(q3, "M3", T.M[:, 768:1024], l3, 4095, OP.bitwise_and)

    def init_pockets():
        ts("PK", "SH", T.SH[:], T.PK[:], 12, OP.logical_shift_right)
        ts("PK", "M0 M1 M2 M3", T.M[:], T.PK[:], 4095, OP.bitwise_and)
        for i in range(4):
            s = slice(256 * i, 256 * i + 256)
            ts("SH", "b6", hi(T.b6), T.SH[:, s], 12288.0, OP.mult, 4096.0 * (3 - i), OP.add)
            tt("PK b6", "Q%d" % i, T.Q[:, s], T.PK[:, s], hi(T.b6), OP.add)

    def finish_pockets():
        ts("Q0 Q1 Q2", "SH", T.SH[:, 0:768], T.Q[:, 0:768], 14, OP.logical_shift_right)
        for i in range(3):
            s = slice(256 * i, 256 * i + 256)
            b = ("b0", "b1", "b2")[i]
            ts("SH", b, lo(T[b]), T.SH[:, s], -12288.0, OP.mult, -4096.0 * (3 - i), OP.add)
            tt("Q%d " % i + b, "OUTP%d" % i, T.OUTP[:, s], T.Q[:, s], lo(T[b]), OP.add)
        D("s", "oq", "OUTP0 OUTP1 OUTP2", "YP", T.yp[:, 0:768], T.OUTP[:])

    def sel(i, t):
        s = slice(256 * i, 256 * i + 256)
        eq = [T.EQ[:, 256 * j:256 * j + 256] for j in range(4)]
        b, o = (("b6", lo(T.b6)), ("b6", hi(T.b6)), ("b4", lo(T.b4)))[i]
        mm("ID8 EQ%d" % i, b, o, T.ID8[:], eq[i], True, False)
        for j in range(4):
            if j < i:
                mm("NID16 EQ%d" % j, b, o, T.NID16[:], eq[j], False, False)
            elif j > i:
                mm("NID EQ%d" % j, b, o, T.NID[:], eq[j], False, False)
        mm("ID GI%d" % i, b, o, T.ID[:], T.GI[:, s], False, True)
        if t == 2:
            act(b, b, o, o, AF.Relu)
            act(b, "SL%d" % i, T.SL[:, s], o, AF.Sign)
        else:
            held.append(lambda: ts(b, "SL%d" % i, T.SL[:, s], o, 0.5, OP.is_ge))

    def update(t):
        at = (("b0", lo(T.b0)), ("b0", hi(T.b0)), ("b1", lo(T.b1)))
        for i, (b, o) in enumerate(at):
            tt("Q%d " % i + b, b, o, o, T.Q[:, 256 * i:256 * i + 256], OP.subtract)
        for i, (b, o) in enumerate(at):
            s = slice(256 * i, 256 * i + 256)
            if held:
                held.pop(0)()
            tt("SL%d " % i + b, b, o, T.SL[:, s], o, OP.mult)
            tt("Q%d " % i + b, "Q%d" % i, T.Q[:, s], T.Q[:, s], o, OP.add)
            if t < 2:
                ts("Q%d" % i, "M%d" % i, T.M[:, s], T.Q[:, s], 4095, OP.bitwise_and)

    def wrap():
        tt("TA b3", "b4", hi(T.b4), T.TA[:], lo(T.b3), OP.is_gt)

    cp("JM", "J0", T.J0[:], T.JM[:])
    ts("JT", "TT", T.TT[:], T.JT[:], 4095, OP.bitwise_and)
    gather_tools(0)
    gather_jobs(0)
    act("ID", "NID", T.NID[:], T.ID[:], scale=-1.0)
    for c in range(4):
        gather_d(c)
        flush_d()
    act("LM J0", "LJ", T.LJ[:], T.LM[:].indirect(T.J0[:]))
    for nm, f in (("ID8", 8.0), ("NID16", -16.0), ("IDQ", 16384.0), ("IDM", -1408.0), ("IDW", 3072.0)):
        act("ID", nm, T[nm][:], T.ID[:], scale=f)

    def first(x):
        if x == 0:
            for c in range(4):
                gather_n(c, 0)
            wrap()
            ts("PI", "PG", T.PG[:], T.PI[:], 112, OP.bitwise_and)
            tt("PG KI", "CK", T.CK[:], T.PG[:], T.KI[:], OP.add)
            ts("ROW8 CK", "IB", T.IB[:], T.ROW8[:], T.CK[:, 0:1], OP.is_equal, 16.0, OP.mult)
            ts("RT", "RTF", T.RTF[:, 0:3], T.RT[:, 0:3], -1.0, OP.mult, 255.0, OP.add)
            for t in range(3):
                ts("PQ", "THR", T.THR[:, t:t + 1], T.PQ[:, 0:1], KDS[t] - 0.5, OP.is_ge, 8.0, OP.mult)
        elif x == 1:
            init_pockets()
        else:
            victims(0)
    wear(0, first)

    for t in range(3):
        last = t == 2
        J, J2 = "J%d" % (t % 2), "J%d" % ((t + 1) % 2)
        ac, nf = "AC%d" % (t % 2), "NF%d" % (t % 2)

        def tool(b, o, first, stop):
            mm("ID " + ac, b, o, T.ID[:], T[ac][:], first, False)
            mm("ID CP", b, o, T.ID[:], T.CP[:], False, False)
            mm("IDM COND", b, o, T.IDM[:], T.COND[:], False, False)
            mm("ID CD", b, o, T.ID[:], T.CD[:], False, False)
            mm("IDW CW", b, o, T.IDW[:], T.CW[:], False, stop)
        ts("b2 THR", "COND", T.COND[:], lo(T.b2), T.THR[:, t:t + 1], OP.is_gt)
        tt("COND b3", "CN", T.CN[:], T.COND[:], hi(T.b3), OP.mult)
        mm("ID " + nf, "b6", hi(T.b6), T.ID[:], T[nf][:], True, False)
        mm("ID CN", "b6", hi(T.b6), T.ID[:], T.CN[:], False, True)
        act("b6", "NN", T.NN[:], hi(T.b6))
        tt("COND b3", "CD", T.CD[:], T.COND[:], lo(T.b3), OP.mult)
        tt("COND b4", "CW", T.CW[:], T.COND[:], hi(T.b4), OP.mult)
        tool("b6", lo(T.b6), True, True)
        if not last:
            tt("NN b5", "NH", T.NH[:], T.NN[:], lo(T.b5), OP.mult)
        tt("MC b5", "G1", T.G1[:], T.MC[:], lo(T.b5), OP.mult)
        for i in range(4):
            tt("M%d b6" % i, "EQ%d" % i, T.EQ[:, 256 * i:256 * i + 256], T.M[:, 256 * i:256 * i + 256], lo(T.b6), OP.is_equal)
        act("b6 BB", "UC", T.UC[:], lo(T.b6), AF.Identity, bias=T.BB[:, 3:4])
        if not last:
            act("b6", "UU", T.UU[:], lo(T.b6))
            list_of("NH", T.NH, 288)
        for i in range(4):
            mm("ID EQ%d" % i, "b2", hi(T.b2), T.ID[:], T.EQ[:, 256 * i:256 * i + 256], i == 0, i == 3)
        if not last:
            cp("b7", J2, T[J2][:], T.b7[:, 288:304])
        tt("H b2", "b5", hi(T.b5), T.H[:], hi(T.b2), OP.min)
        tt("MC b5", "G3", T.G3[:], T.MC[:], hi(T.b5), OP.mult)
        tt("UC b5", "G2", T.G2[:], T.UC[:], hi(T.b5), OP.mult)
        act("b5", "HH", T.HH[:], hi(T.b5))
        act("b2 BB", "b2", lo(T.b2), hi(T.b2), AF.Relu, scale=-BIG, bias=T.BB[:, 4:5])
        mm("BLK G1", "b7", lo(T.b7), T.BLK[:], T.G1[:], True, False)
        mm("NBLK G3", "b7", lo(T.b7), T.NBLK[:], T.G3[:], False, False)
        mm("BLK G2", "b7", lo(T.b7), T.BLK[:], T.G2[:], False, True)
        mm("BLK HH", "b2", hi(T.b2), T.BLK[:], T.HH[:], True, True)
        if not last:
            cp("UU " + J, "TT", T.TT[:].indirect(T[J][:]), T.UU[:])
        cp("b7", "VR", T.VR[:], lo(T.b7))
        list_of("VR", T.VR, 256)
        act("b2", "UP", T.UP[:], hi(T.b2))

        def give():
            q3, l3 = pocket3(t)
            tt(q3 + " b2", "b2", lo(T.b2), l3, lo(T.b2), OP.max)
            tt("EV b2", "S1", T.S1[:], T.EV[:], lo(T.b2), OP.min)
            sb = "SB%d" % t
            if not last:
                ts("S1", sb, T[sb][:], T.S1[:], 0xFFCFFF, OP.bitwise_and)
            else:
                ts("S1", "IX", T.IX[:], T.S1[:], 14, OP.logical_shift_right)
                ts("S1", "S2", T.S2[:], T.S1[:], 0xFFCFFF, OP.bitwise_and)
                ts("IX", "b2", lo(T.b2), T.IX[:], -12288.0, OP.mult)
                tt("S2 b2", sb, T[sb][:], T.S2[:], lo(T.b2), OP.add)
            rid, pid = topo.addr(nxt)[0:2]
            emit("g", lambda: g.remote_dma(out_ap=T["LAND%d" % (t + 1)][:], in_ap=T[sb][:], remote_sem=T.sem["ar%d" % t], local_sem=T.sem["lc%d" % t],
                                           pid=pid, routing_id=rid, dma_engine_mask=topo.mask(core, nxt)),
                 [sb], [], "lc%d" % t, 0, len(topo.engines(core, nxt)))
            wrote["LAND%d" % (t + 1)] = ("ar%d" % t, len(topo.engines(prv, core)))
        if not last:
            gather_tools(t + 1)
            gather_d(0)
            cp("NN " + J, "NT", T.NT[:].indirect(T[J][:]), T.NN[:])
        else:
            give()
        ts("b7", "VL", T.VL[:], T.b7[:, 256:272], 0.0625, OP.mult, 1664.0, OP.add)
        ts("b7", "VLF", T.VLF[:], T.b7[:, 256:272], 0.0625, OP.mult)
        for q in range(16):
            ts("VR VLF", "E%d" % q, T.E[:, 256 * q + 16 * q:256 * q + 256], T.VR[:, 16 * q:256], T.VLF[:, q:q + 1], OP.is_equal)
        act("X VL EB", "Y2", T.Y2[:], T.X[:, 0:3072].indirect(T.VL[:]), AF.Relu, bias=T.EB[:])
        act("X VL RTF", "Y1", T.Y1[:], T.X[:, 0:3072].indirect(T.VL[:]), AF.Relu, scale=-1.0, bias=T.RTF[:, t:t + 1])
        mm("IDQ " + nf, "b1", hi(T.b1), T.IDQ[:], T[nf][:], True, False)
        mm("IDQ CN", "b1", hi(T.b1), T.IDQ[:], T.CN[:], False, False)
        tool("b1", hi(T.b1), False, True)
        mm("ID CQ", "b5", lo(T.b5), T.ID[:], T.CQ[:], True, False)
        for q in range(15):
            mm("BLKQ E%d" % q, "b5", T.b5[:, 16 * q + 16:256], T.BLKQ[:], T.E[:, 256 * q + 16 * q + 16:256 * q + 256], False, False)
        ee = " ".join("E%d" % q for q in range(16))
        for r in range(1, 16):
            mm("LT " + ee, "b5", T.b5[:, r:256:16], T.LT[:, r, :], T.E[:, r::272], False, r == 15)
        if not last:
            give()
        tt("CM b5", "YM", T.YM[:], T.CM[:], lo(T.b5), OP.min)
        tt("YM b7", "OF", T.OF[:], T.YM[:], lo(T.b7), OP.max)
        mm("ID C255", "b5", hi(T.b5), T.ID[:], T.C255[:], True, False)
        mm("NID Y1", "b5", hi(T.b5), T.NID[:], T.Y1[:], False, False)
        mm("NID Y2", "b5", hi(T.b5), T.NID[:], T.Y2[:], False, True)
        list_of("OF", T.OF, 272)
        if not last:
            gather_jobs(t + 1)
        tt("UP b5", "YT", T.YT[:], T.UP[:], hi(T.b5), OP.mult)
        if not last:
            gather_d(1)
        for i in range(3):
            b, o = (("b0", lo(T.b0)), ("b0", hi(T.b0)), ("b1", lo(T.b1)))[i]
            act("b1 BB", b, o, hi(T.b1), AF.Identity, bias=T.BB[:, i:i + 1])
        ts("b7", "OL", T.OL[:], T.b7[:, 272:288], 0.0625, OP.mult, 1664.0, OP.add)
        V("Y2 YT OL", "X", lambda: g.vector.tensor_tensor(out=T.X[:].indirect(T.OL[:]), in0=T.Y2[:], in1=T.YT[:], op=OP.add))
        if last:
            D("s", "ox", "X", "YX", T.yx[:, 0:3072], T.X[:, 0:3072])
            for i in range(3):
                sel(i, t)
            update(t)
            finish_pockets()
            D("a", "o3", "LAND3", "YP3", T.yp[:, 768:1024], T.LAND3[:])
        else:
            gather_d(2)
            gather_d(3)

            def fillers(x):
                if x == 0:
                    for i in range(3):
                        sel(i, t)
                    flush_d()
                    update(t)
                    wrap()
                    for c in range(NB):
                        gather_n(c, t + 1)
                elif x == 1:
                    for c in range(NB, 4):
                        gather_n(c, t + 1)
                else:
                    victims(t + 1)
            wear(t + 1, fillers)
    for s in ("sv", "sa", "st", "sg"):
        g.wait_ge(T.sem[s], count[s])
    for d in DMAS:
        g.wait_ge(T.sem["d" + d], 16)
    for t in range(3):
        g.wait_ge(T.sem["lc%d" % t], len(topo.engines(core, nxt)))
        g.wait_ge(T.sem["ar%d" % t], len(topo.engines(prv, core)))
